import numpy as np
import ml_dtypes


def mxq(x, axis, fmt="e4m3"):
    dtype, down = {"e4m3": (ml_dtypes.float8_e4m3fn, 7), "e5m2": (ml_dtypes.float8_e5m2, 14)}[fmt]
    v = np.moveaxis(np.asarray(x, np.float32).astype(ml_dtypes.bfloat16).astype(np.float64), axis, -1)
    blocks = v.reshape(v.shape[:-1] + (-1, 32))
    amax = np.abs(blocks).max(-1, keepdims=True)
    byte = np.maximum(np.where(amax > 0, np.frexp(amax)[1] - 1 + 127, 0) - down, 1)
    scale = np.exp2(byte - 127.0)
    codes = (blocks / scale).astype(np.float32).astype(dtype).astype(np.float64)
    return np.moveaxis((codes * scale).reshape(v.shape), -1, axis)


WIDE = False


def mx_kscale(k):
    if not WIDE:
        return np.ones(k)
    levels = np.array([10, -10, 5, -5, 0])
    if k % 512:
        return np.exp2(np.random.permutation(np.resize(levels, k // 32))).repeat(32)
    a = np.empty((k // 512, 16))
    for p in range(k // 512):
        a[p, :8] = np.random.permutation(np.resize(levels, 8))
        for g in range(8):
            far = levels[np.abs(levels - a[p, g]) >= 10]
            a[p, g + 8] = far[np.random.randint(len(far))]
    return np.exp2(a.ravel()).repeat(32)


def f64(x):
    return np.asarray(x).astype(np.float64)


def striped(idx):
    return np.tile(idx.reshape(-1, 16).T, (8, 1)).astype(np.uint16)


def unstriped(offs):
    return offs[:16].T.reshape(-1).astype(np.int64)


E2M1 = np.array([0.0, 0.5, 1.0, 1.5, 2.0, 3.0, 4.0, 6.0, -0.0, -0.5, -1.0, -1.5, -2.0, -3.0, -4.0, -6.0])


def pack_weight(w, fmt):
    k, n = w.shape
    w = f64(np.asarray(w, np.float32).astype(ml_dtypes.bfloat16)).reshape(k // 32, 32, n)
    amax = np.abs(w).max(1)
    if fmt == "e4m3":
        byte = np.frexp(amax)[1] - 1 + 127 - 7
    else:
        mant, ex = np.frexp(amax / 6.0)
        byte = np.where(mant > 0.5, ex, ex - 1) + 127
    byte = np.clip(np.where(amax > 0, byte, 1), 1, 254)
    scaled = (w * np.exp2(127.0 - byte)[:, None, :]).reshape(k, n).astype(np.float32)
    by_word = np.ascontiguousarray(scaled.reshape(k // 512, 128, 4, n).transpose(0, 1, 3, 2))
    if fmt == "e4m3":
        words = by_word.astype(ml_dtypes.float8_e4m3fn).view(np.uint8)
    else:
        c = by_word.astype(ml_dtypes.float4_e2m1fn).view(np.uint8) & 0xF
        words = (c[..., 0::2] | (c[..., 1::2] << 4)).reshape(k // 512, 128, 2 * n)
    return np.ascontiguousarray(words), np.ascontiguousarray(byte.astype(np.uint8).reshape(k // 512, 16, n))


def unpack_weight(words, scales, fmt):
    g, _, n = scales.shape
    words = np.ascontiguousarray(words).reshape(g, 128, n, -1)
    if fmt == "e4m3":
        vals = words.view(ml_dtypes.float8_e4m3fn).astype(np.float64)
    else:
        nib = np.empty((g, 128, n, 4), np.uint8)
        nib[..., 0::2] = words & 0xF
        nib[..., 1::2] = words >> 4
        vals = E2M1[nib]
    vals = vals * np.repeat(np.exp2(scales.astype(np.float64) - 127.0), 8, axis=1)[..., None]
    return vals.transpose(0, 1, 3, 2).reshape(g * 512, n)


def split(x):
    m, e = np.frexp(f64(x))
    hi = np.ldexp(np.trunc(16.0 * m) / 16.0, e)
    return hi, f64(x) - hi


def gelu(v):
    return 0.5 * v * (1.0 + np.tanh(np.sqrt(2.0 / np.pi) * (v + 0.044715 * v**3)))


K, M, T, S = 1024, 128, 4096, 2048


def setup_inputs():
    n = np.random.standard_normal
    s = mx_kscale(K)[:, None]
    v = pack_weight(n((K, T)) * s, "e4m3")
    return {
        "tab_words": v[0],
        "tab_scales": v[1],
        "w": (n((K, M)) / np.sqrt(K) / s).astype(np.float32),
        "rT": n((M, T)).astype(np.float32),
        "b": (0.3 * n(128)).astype(np.float32),
        "offs": striped(np.random.permutation(T)[:S]),
    }


def reference(tab_words, tab_scales, w, rT, b, offs):
    tab_ = unpack_weight(tab_words, tab_scales, "e4m3")[:, unstriped(offs)]
    w_hi, w_lo = split(w)
    w_hi_, w_lo_ = mxq(w_hi, 0, "e4m3"), mxq(w_lo, 0, "e4m3")
    y = w_hi_.T @ tab_ + w_lo_.T @ tab_
    return (gelu(y + f64(b)[:, None])) + f64(rT)[:, unstriped(offs)]

@@ -1,0 +1,119 @@
+from contextlib import ExitStack
+
+import concourse.mybir as mybir
+
+K, M, T, S = 1024, 128, 4096, 2048
+FLOPS = 2 * 2 * K * M * S
+BYTES = K * T + (K // 32) * T + 4 * K * M + 4 * M * T + 4 * M + 2 * 128 * (S // 16) + 4 * M * S
+
+F32 = mybir.dt.float32
+BF16 = mybir.dt.bfloat16
+I32 = mybir.dt.int32
+U32 = mybir.dt.uint32
+U16 = mybir.dt.uint16
+U8 = mybir.dt.uint8
+FP8X4 = mybir.dt.float8_e4m3fn_x4
+ALU = mybir.AluOpType
+ACT = mybir.ActivationFunctionType
+
+P = 128
+PACK = 4
+PASSES = K // (P * PACK)
+BANK = 512
+HI_MASK = 0xFFF0FFF0 - (1 << 32)
+GATHER_WIDTH = (1024, 512)
+OUT_WIDTHS = (512, 512, 512, 256, 256)
+
+
+def tile_list_tabres_gelu_kernel(tc, tab_words, tab_scales, w, rT, b, offs, out):
+    nc = tc.nc
+    with ExitStack() as ctx:
+        keep = ctx.enter_context(tc.tile_pool(name="keep", bufs=1))
+        psum = ctx.enter_context(tc.psum_pool(name="psum", bufs=1))
+
+        offsets = keep.tile([P, S // 16], U16, name="offsets")
+        nc.sync.dma_start(offsets[:], offs)
+
+        def entries(lo, width):
+            return offsets[:, lo // 16 : (lo + width) // 16]
+
+        scale_table = keep.tile([P, T], U8, name="scale_table")
+        nc.sync.dma_start(
+            scale_table[0:32, :].bitcast(I32),
+            tab_scales.rearrange("a q t -> (a q) t").bitcast(I32),
+        )
+        nc.vector.memset(scale_table[32:64, :].bitcast(I32), 0)
+        nc.vector.memset(scale_table[64:128, :].bitcast(I32), 0)
+
+        w_raw = keep.tile([P, PASSES, PACK, M], F32, name="w_raw", tag="w_raw_then_planes", align_bytes=64)
+        nc.sync.dma_start(w_raw[:], w.rearrange("(a p i) n -> p a i n", a=PASSES, i=PACK))
+        word_tables = []
+        for a in range(PASSES):
+            table = keep.tile([P, T], I32, name="word_table%d" % a)
+            nc.sync.dma_start(table[:], tab_words[a].rearrange("p t i -> p (t i)").bitcast(I32))
+            word_tables.append(table)
+        residual = keep.tile([P, T], F32, name="residual")
+        nc.sync.dma_start(residual[:], rT)
+        bias = keep.tile([P, 1], F32, name="bias")
+        nc.gpsimd.dma_start(bias[:], b.rearrange("(p o) -> p o", o=1))
+
+        picked_scales = keep.tile([P, S], U8, name="picked_scales")
+        nc.vector.tensor_copy(picked_scales[:], scale_table[:].indirect(offsets[:]))
+
+        half = PASSES * M * PACK
+        w_woven = keep.tile([P, half], F32, name="w_woven")
+        nc.scalar.copy(
+            w_woven[:].rearrange("p (a n i) -> p a n i", a=PASSES, i=PACK),
+            w_raw[:].rearrange("p a i n -> p a n i"),
+        )
+        w_top = keep.tile([P, half], BF16, name="w_top")
+        nc.scalar.copy(w_top[:], w_woven[:].bitcast(BF16)[:, 1 : 2 * half : 2])
+        planes = keep.tile([P, S], U8, name="planes", tag="w_raw_then_planes", align_bytes=64)
+        nc.gpsimd.memset(planes[:].bitcast(I32), 0)
+        for a, queue in enumerate((nc.scalar, nc.gpsimd)):
+            for quad in range(4):
+                src = 16 * a + 4 * quad
+                dst = 32 * quad + 4 * a
+                queue.dma_start(planes[dst : dst + 4, :].bitcast(I32), picked_scales[src : src + 4, :].bitcast(I32))
+
+        parts = keep.tile([P, 2 * half], BF16, name="parts", align_bytes=64)
+        nc.vector.tensor_scalar(parts[:, :half].bitcast(I32), w_top[:].bitcast(I32), HI_MASK, None, ALU.bitwise_and)
+        nc.vector.tensor_tensor(parts[:, half:], w_woven[:], parts[:, :half], ALU.subtract)
+        w_codes = keep.tile([P, 2 * PASSES * M], U32, name="w_codes", align_bytes=64)
+        w_scales = keep.tile([P, 2 * PASSES * M], U8, name="w_scales", align_bytes=64)
+        nc.vector.quantize_mx(
+            out=w_codes[:].bitcast(FP8X4), scales=w_scales[:], in_=parts[:]
+        )
+
+        banks = [psum.tile([M, BANK], F32, name="bank%d" % c) for c in range(S // BANK)]
+        activated = [keep.tile([M, BANK], F32, name="activated%d" % c) for c in range(S // BANK)]
+        for a in range(PASSES):
+            width = GATHER_WIDTH[a]
+            for lo in range(0, S, width):
+                picked = keep.tile([P, width], U32, name="picked%d_%d" % (a, lo), align_bytes=64)
+                nc.vector.tensor_copy(picked[:], word_tables[a][:].bitcast(U32).indirect(entries(lo, width)))
+                for col in range(lo, lo + width, BANK):
+                    c = col // BANK
+                    for part in range(2):
+                        w_cols = slice((part * PASSES + a) * M, (part * PASSES + a + 1) * M)
+                        nc.tensor.matmul_mx(
+                            out=banks[c][:],
+                            lhsT=w_codes[:, w_cols].bitcast(FP8X4),
+                            lhsT_scale=w_scales[:, w_cols],
+                            rhs=picked[:, col - lo : col - lo + BANK].bitcast(FP8X4),
+                            rhs_scale=planes[4 * a : P, col : col + BANK],
+                            start=(a == 0 and part == 0),
+                            stop=(a == PASSES - 1 and part == 1),
+                        )
+                    if a == PASSES - 1:
+                        nc.scalar.activation(activated[c][:], banks[c][:], ACT.Gelu_apprx_tanh, bias=bias[:])
+
+        lo = 0
+        for width in OUT_WIDTHS:
+            c, inner = divmod(lo, BANK)
+            result = keep.tile([M, width], F32, name="result%d" % lo)
+            nc.vector.tensor_tensor(
+                result[:], residual[:].indirect(entries(lo, width)), activated[c][:, inner : inner + width], ALU.add
+            )
+            nc.sync.dma_start(out[:, lo : lo + width], result[:])
+            lo = lo + width

@@ -38,27 +38,34 @@ def tile_list_tabres_gelu_kernel(tc, tab_words, tab_scales, w, rT, b, offs, out)
             return offsets[:, lo // 16 : (lo + width) // 16]
 
         scale_table = keep.tile([P, T], U8, name="scale_table")
-        nc.sync.dma_start(
-            scale_table[0:32, :].bitcast(I32),
-            tab_scales.rearrange("a q t -> (a q) t").bitcast(I32),
-        )
+        for a in range(PASSES):
+            nc.sync.dma_start(
+                scale_table[16 * a : 16 * a + 16, :].bitcast(I32),
+                tab_scales[a].bitcast(I32).rearrange("(q r) t -> r q t", r=4),
+            )
         nc.vector.memset(scale_table[32:64, :].bitcast(I32), 0)
         nc.vector.memset(scale_table[64:128, :].bitcast(I32), 0)
+        planes = keep.tile([P, S], U8, name="planes", align_bytes=64)
+        nc.vector.memset(planes[:].bitcast(I32), 0)
 
-        w_raw = keep.tile([P, PASSES, PACK, M], F32, name="w_raw", tag="w_raw_then_planes", align_bytes=64)
-        nc.sync.dma_start(w_raw[:], w.rearrange("(a p i) n -> p a i n", a=PASSES, i=PACK))
-        word_tables = []
-        for a in range(PASSES):
-            table = keep.tile([P, T], I32, name="word_table%d" % a)
-            nc.sync.dma_start(table[:], tab_words[a].rearrange("p t i -> p (t i)").bitcast(I32))
-            word_tables.append(table)
+        word_tables = [keep.tile([P, T], I32, name="word_table%d" % a) for a in range(PASSES)]
+        w_raw = keep.tile([P, PASSES, PACK, M], F32, name="w_raw")
         residual = keep.tile([P, T], F32, name="residual")
+        nc.sync.dma_start(word_tables[0][:], tab_words[0].rearrange("p t i -> p (t i)").bitcast(I32))
+        nc.sync.dma_start(w_raw[:], w.rearrange("(a p i) n -> p a i n", a=PASSES, i=PACK))
+        nc.sync.dma_start(word_tables[1][:], tab_words[1].rearrange("p t i -> p (t i)").bitcast(I32))
         nc.sync.dma_start(residual[:], rT)
         bias = keep.tile([P, 1], F32, name="bias")
-        nc.gpsimd.dma_start(bias[:], b.rearrange("(p o) -> p o", o=1))
+        nc.scalar.dma_start(bias[:], b.rearrange("(p o) -> p o", o=1))
+        warm = keep.tile([P, 1], F32, name="warm")
+        nc.scalar.activation(warm[:], bias[:], ACT.Gelu_apprx_tanh, bias=bias[:])
 
         picked_scales = keep.tile([P, S], U8, name="picked_scales")
         nc.vector.tensor_copy(picked_scales[:], scale_table[:].indirect(offsets[:]))
+        for quad in range(4):
+            nc.scalar.dma_start(
+                planes[32 * quad : 32 * quad + 8, :].bitcast(I32), picked_scales[quad:32:4, :].bitcast(I32)
+            )
 
         half = PASSES * M * PACK
         w_woven = keep.tile([P, half], F32, name="w_woven")
@@ -68,14 +75,6 @@ def tile_list_tabres_gelu_kernel(tc, tab_words, tab_scales, w, rT, b, offs, out)
         )
         w_top = keep.tile([P, half], BF16, name="w_top")
         nc.scalar.copy(w_top[:], w_woven[:].bitcast(BF16)[:, 1 : 2 * half : 2])
-        planes = keep.tile([P, S], U8, name="planes", tag="w_raw_then_planes", align_bytes=64)
-        nc.gpsimd.memset(planes[:].bitcast(I32), 0)
-        for a, queue in enumerate((nc.scalar, nc.gpsimd)):
-            for quad in range(4):
-                src = 16 * a + 4 * quad
-                dst = 32 * quad + 4 * a
-                queue.dma_start(planes[dst : dst + 4, :].bitcast(I32), picked_scales[src : src + 4, :].bitcast(I32))
-
         parts = keep.tile([P, 2 * half], BF16, name="parts", align_bytes=64)
         nc.vector.tensor_scalar(parts[:, :half].bitcast(I32), w_top[:].bitcast(I32), HI_MASK, None, ALU.bitwise_and)
         nc.vector.tensor_tensor(parts[:, half:], w_woven[:], parts[:, :half], ALU.subtract)

@@ -37,35 +37,32 @@ def tile_list_tabres_gelu_kernel(tc, tab_words, tab_scales, w, rT, b, offs, out)
         def entries(lo, width):
             return offsets[:, lo // 16 : (lo + width) // 16]
 
-        scale_table = keep.tile([P, T], U8, name="scale_table")
+        scale_table = keep.tile([P, T], U8, name="scale_table", tag="scales_then_residual")
         for a in range(PASSES):
             nc.sync.dma_start(
-                scale_table[16 * a : 16 * a + 16, :].bitcast(I32),
+                scale_table[96 + 16 * a : 112 + 16 * a, :].bitcast(I32),
                 tab_scales[a].bitcast(I32).rearrange("(q r) t -> r q t", r=4),
             )
-        nc.vector.memset(scale_table[32:64, :].bitcast(I32), 0)
-        nc.vector.memset(scale_table[64:128, :].bitcast(I32), 0)
+        nc.vector.memset(scale_table[0:96, :].bitcast(I32), 0)
         planes = keep.tile([P, S], U8, name="planes", align_bytes=64)
         nc.vector.memset(planes[:].bitcast(I32), 0)
 
         word_tables = [keep.tile([P, T], I32, name="word_table%d" % a) for a in range(PASSES)]
         w_raw = keep.tile([P, PASSES, PACK, M], F32, name="w_raw")
-        residual = keep.tile([P, T], F32, name="residual")
-        nc.sync.dma_start(word_tables[0][:], tab_words[0].rearrange("p t i -> p (t i)").bitcast(I32))
         nc.sync.dma_start(w_raw[:], w.rearrange("(a p i) n -> p a i n", a=PASSES, i=PACK))
-        nc.sync.dma_start(word_tables[1][:], tab_words[1].rearrange("p t i -> p (t i)").bitcast(I32))
-        nc.sync.dma_start(residual[:], rT)
+        for a in range(PASSES):
+            nc.sync.dma_start(word_tables[a][:], tab_words[a].rearrange("p t i -> p (t i)").bitcast(I32))
         bias = keep.tile([P, 1], F32, name="bias")
-        nc.scalar.dma_start(bias[:], b.rearrange("(p o) -> p o", o=1))
-        warm = keep.tile([P, 1], F32, name="warm")
-        nc.scalar.activation(warm[:], bias[:], ACT.Gelu_apprx_tanh, bias=bias[:])
+        nc.sync.dma_start(bias[:], b.rearrange("(p o) -> p o", o=1))
 
         picked_scales = keep.tile([P, S], U8, name="picked_scales")
         nc.vector.tensor_copy(picked_scales[:], scale_table[:].indirect(offsets[:]))
         for quad in range(4):
-            nc.scalar.dma_start(
-                planes[32 * quad : 32 * quad + 8, :].bitcast(I32), picked_scales[quad:32:4, :].bitcast(I32)
+            nc.sync.dma_start(
+                planes[32 * quad : 32 * quad + 8, :].bitcast(I32), picked_scales[96 + quad : P : 4, :].bitcast(I32)
             )
+        residual = keep.tile([P, T], F32, name="residual", tag="scales_then_residual")
+        nc.sync.dma_start(residual[:], rT)
 
         half = PASSES * M * PACK
         w_woven = keep.tile([P, half], F32, name="w_woven")

@@ -1,6 +1,7 @@
 from contextlib import ExitStack
 
 import concourse.mybir as mybir
+from concourse.masks import make_identity
 
 K, M, T, S = 1024, 128, 4096, 2048
 FLOPS = 2 * 2 * K * M * S
@@ -20,8 +21,8 @@ P = 128
 PACK = 4
 PASSES = K // (P * PACK)
 BANK = 512
-HI_MASK = 0xFFF0FFF0 - (1 << 32)
-GATHER_WIDTH = (1024, 512)
+HI_MASK = -(1 << 20)
+SIGN_BIT = -(1 << 31)
 OUT_WIDTHS = (512, 512, 512, 256, 256)
 
 
@@ -47,13 +48,18 @@ def tile_list_tabres_gelu_kernel(tc, tab_words, tab_scales, w, rT, b, offs, out)
         planes = keep.tile([P, S], U8, name="planes", align_bytes=64)
         nc.vector.memset(planes[:].bitcast(I32), 0)
 
-        word_tables = [keep.tile([P, T], I32, name="word_table%d" % a) for a in range(PASSES)]
+        word_tables = [
+            keep.tile([P, T], I32, name="word_table%d" % a, tag="word_table%d" % a, align_bytes=64)
+            for a in range(PASSES)
+        ]
         w_raw = keep.tile([P, PASSES, PACK, M], F32, name="w_raw")
         nc.sync.dma_start(w_raw[:], w.rearrange("(a p i) n -> p a i n", a=PASSES, i=PACK))
         for a in range(PASSES):
             nc.sync.dma_start(word_tables[a][:], tab_words[a].rearrange("p t i -> p (t i)").bitcast(I32))
-        bias = keep.tile([P, 1], F32, name="bias")
-        nc.sync.dma_start(bias[:], b.rearrange("(p o) -> p o", o=1))
+        identity = keep.tile([P, P], F32, name="identity")
+        make_identity(nc, identity[:])
+        bias = keep.tile([M, 1], F32, name="bias")
+        nc.sync.dma_start(bias[:], b.rearrange("(n o) -> n o", o=1))
 
         picked_scales = keep.tile([P, S], U8, name="picked_scales")
         nc.vector.tensor_copy(picked_scales[:], scale_table[:].indirect(offsets[:]))
@@ -64,45 +70,63 @@ def tile_list_tabres_gelu_kernel(tc, tab_words, tab_scales, w, rT, b, offs, out)
         residual = keep.tile([P, T], F32, name="residual", tag="scales_then_residual")
         nc.sync.dma_start(residual[:], rT)
 
-        half = PASSES * M * PACK
-        w_woven = keep.tile([P, half], F32, name="w_woven")
-        nc.scalar.copy(
-            w_woven[:].rearrange("p (a n i) -> p a n i", a=PASSES, i=PACK),
-            w_raw[:].rearrange("p a i n -> p a n i"),
-        )
-        w_top = keep.tile([P, half], BF16, name="w_top")
-        nc.scalar.copy(w_top[:], w_woven[:].bitcast(BF16)[:, 1 : 2 * half : 2])
-        parts = keep.tile([P, 2 * half], BF16, name="parts", align_bytes=64)
-        nc.vector.tensor_scalar(parts[:, :half].bitcast(I32), w_top[:].bitcast(I32), HI_MASK, None, ALU.bitwise_and)
-        nc.vector.tensor_tensor(parts[:, half:], w_woven[:], parts[:, :half], ALU.subtract)
-        w_codes = keep.tile([P, 2 * PASSES * M], U32, name="w_codes", align_bytes=64)
-        w_scales = keep.tile([P, 2 * PASSES * M], U8, name="w_scales", align_bytes=64)
-        nc.vector.quantize_mx(
-            out=w_codes[:].bitcast(FP8X4), scales=w_scales[:], in_=parts[:]
-        )
-
-        banks = [psum.tile([M, BANK], F32, name="bank%d" % c) for c in range(S // BANK)]
-        activated = [keep.tile([M, BANK], F32, name="activated%d" % c) for c in range(S // BANK)]
+        w_turned = keep.tile([M, PASSES * BANK], F32, name="w_turned", tag="w_turned_then_picked0", align_bytes=64)
         for a in range(PASSES):
-            width = GATHER_WIDTH[a]
-            for lo in range(0, S, width):
-                picked = keep.tile([P, width], U32, name="picked%d_%d" % (a, lo), align_bytes=64)
-                nc.vector.tensor_copy(picked[:], word_tables[a][:].bitcast(U32).indirect(entries(lo, width)))
-                for col in range(lo, lo + width, BANK):
-                    c = col // BANK
-                    for part in range(2):
-                        w_cols = slice((part * PASSES + a) * M, (part * PASSES + a + 1) * M)
-                        nc.tensor.matmul_mx(
-                            out=banks[c][:],
-                            lhsT=w_codes[:, w_cols].bitcast(FP8X4),
-                            lhsT_scale=w_scales[:, w_cols],
-                            rhs=picked[:, col - lo : col - lo + BANK].bitcast(FP8X4),
-                            rhs_scale=planes[4 * a : P, col : col + BANK],
-                            start=(a == 0 and part == 0),
-                            stop=(a == PASSES - 1 and part == 1),
-                        )
-                    if a == PASSES - 1:
-                        nc.scalar.activation(activated[c][:], banks[c][:], ACT.Gelu_apprx_tanh, bias=bias[:])
+            turned = psum.tile([M, PACK, P], F32, name="turned%d" % a, tag="turn%d" % a)
+            for i in range(PACK):
+                nc.tensor.transpose(turned[:, i, :], w_raw[:, a, i, :], identity[:])
+            nc.scalar.copy(w_turned[:, a * BANK : (a + 1) * BANK], turned[:].rearrange("n i p -> n (i p)"))
+        minus_hi = keep.tile([M, PASSES * BANK], F32, name="minus_hi")
+        nc.vector.tensor_scalar(
+            minus_hi[:].bitcast(I32), w_turned[:].bitcast(I32), HI_MASK, SIGN_BIT, ALU.bitwise_and, ALU.bitwise_xor
+        )
+        parts = keep.tile([P, 2 * PASSES * BANK], BF16, name="parts", tag="parts_then_picked1", align_bytes=64)
+        for a in range(PASSES):
+            lo_sum = psum.tile([P, PACK, M], F32, name="lo_sum%d" % a)
+            hi_back = psum.tile([P, PACK, M], F32, name="hi_back%d" % a, tag="turn%d" % a)
+            for term, source in enumerate((w_turned, minus_hi)):
+                for i in range(PACK):
+                    nc.tensor.matmul(
+                        lo_sum[:, i, :],
+                        source[:, a * BANK + i * P : a * BANK + (i + 1) * P],
+                        identity[:],
+                        start=(term == 0 and i == 0),
+                        stop=(term == 1 and i == PACK - 1),
+                        is_transpose=True,
+                    )
+            for i in range(PACK):
+                nc.tensor.transpose(hi_back[:, i, :], minus_hi[:, a * BANK + i * P : a * BANK + (i + 1) * P], identity[:])
+            hi_cols = parts[:, a * BANK : (a + 1) * BANK].rearrange("p (n i) -> p n i", i=PACK)
+            lo_cols = parts[:, (PASSES + a) * BANK : (PASSES + a + 1) * BANK].rearrange("p (n i) -> p n i", i=PACK)
+            nc.scalar.copy(lo_cols, lo_sum[:].rearrange("p i n -> p n i"))
+            nc.scalar.activation(hi_cols, hi_back[:].rearrange("p i n -> p n i"), ACT.Copy, scale=-1.0)
+
+        picked0 = keep.tile([P, S], U32, name="picked0", tag="w_turned_then_picked0", align_bytes=64)
+        nc.vector.tensor_copy(picked0[:], word_tables[0][:].bitcast(U32).indirect(offsets[:]))
+        w_codes = keep.tile([P, 2 * PASSES * M], U32, name="w_codes", tag="word_table0", align_bytes=64)
+        w_scales = keep.tile([P, 2 * PASSES * M], U8, name="w_scales", align_bytes=64)
+        nc.vector.quantize_mx(out=w_codes[:].bitcast(FP8X4), scales=w_scales[:], in_=parts[:])
+
+        picked1 = keep.tile([P, S], U32, name="picked1", tag="parts_then_picked1", align_bytes=64)
+        activated = []
+        for col in range(0, S, BANK):
+            nc.vector.tensor_copy(picked1[:, col : col + BANK], word_tables[1][:].bitcast(U32).indirect(entries(col, BANK)))
+            acc = psum.tile([M, BANK], F32, name="acc%d" % col)
+            for a, picked in enumerate((picked0, picked1)):
+                for part in range(2):
+                    w_cols = slice((part * PASSES + a) * M, (part * PASSES + a + 1) * M)
+                    nc.tensor.matmul_mx(
+                        out=acc[:],
+                        lhsT=w_codes[:, w_cols].bitcast(FP8X4),
+                        lhsT_scale=w_scales[:, w_cols],
+                        rhs=picked[:, col : col + BANK].bitcast(FP8X4),
+                        rhs_scale=planes[4 * a : P, col : col + BANK],
+                        start=(a == 0 and part == 0),
+                        stop=(a == PASSES - 1 and part == 1),
+                    )
+            gelu = keep.tile([M, BANK], F32, name="gelu%d" % col)
+            nc.scalar.activation(gelu[:], acc[:], ACT.Gelu_apprx_tanh, bias=bias[:])
+            activated.append(gelu)
 
         lo = 0
         for width in OUT_WIDTHS:

@@ -21,8 +21,14 @@ P = 128
 PACK = 4
 PASSES = K // (P * PACK)
 BANK = 512
+GROUP = 16
+QUADRANT = 32
+QUAD_ROWS = 4
+PASS_ROWS = 16
+FIRST_ROW = P - PASSES * PASS_ROWS
 HI_MASK = -(1 << 20)
 SIGN_BIT = -(1 << 31)
+MOVE_ORDER = (0, 2, 1, 3)
 OUT_WIDTHS = (512, 512, 512, 256, 256)
 
 
@@ -32,40 +38,39 @@ def tile_list_tabres_gelu_kernel(tc, tab_words, tab_scales, w, rT, b, offs, out)
         keep = ctx.enter_context(tc.tile_pool(name="keep", bufs=1))
         psum = ctx.enter_context(tc.psum_pool(name="psum", bufs=1))
 
-        offsets = keep.tile([P, S // 16], U16, name="offsets")
+        offsets = keep.tile([P, S // GROUP], U16, name="offsets")
         nc.sync.dma_start(offsets[:], offs)
 
-        def entries(lo, width):
-            return offsets[:, lo // 16 : (lo + width) // 16]
+        def entries(first, count):
+            return offsets[:, first // GROUP : (first + count) // GROUP]
 
         scale_table = keep.tile([P, T], U8, name="scale_table", tag="scales_then_residual")
         for a in range(PASSES):
+            first = FIRST_ROW + PASS_ROWS * a
             nc.sync.dma_start(
-                scale_table[96 + 16 * a : 112 + 16 * a, :].bitcast(I32),
-                tab_scales[a].bitcast(I32).rearrange("(q r) t -> r q t", r=4),
+                scale_table[first : first + PASS_ROWS, :].bitcast(I32),
+                tab_scales[a].bitcast(I32).rearrange("(q r) t -> r q t", r=QUAD_ROWS),
             )
-        nc.vector.memset(scale_table[0:96, :].bitcast(I32), 0)
-        planes = keep.tile([P, S], U8, name="planes", align_bytes=64)
-        nc.vector.memset(planes[:].bitcast(I32), 0)
+        nc.vector.memset(scale_table[0:FIRST_ROW, :].bitcast(I32), 0)
+        v_scales = keep.tile([P, S], U8, name="v_scales", align_bytes=64)
+        nc.vector.memset(v_scales[:].bitcast(I32), 0)
 
-        word_tables = [
-            keep.tile([P, T], I32, name="word_table%d" % a, tag="word_table%d" % a, align_bytes=64)
-            for a in range(PASSES)
-        ]
+        word_tables = [keep.tile([P, T], I32, name="word_table%d" % a) for a in range(PASSES)]
         w_raw = keep.tile([P, PASSES, PACK, M], F32, name="w_raw")
         nc.sync.dma_start(w_raw[:], w.rearrange("(a p i) n -> p a i n", a=PASSES, i=PACK))
         for a in range(PASSES):
             nc.sync.dma_start(word_tables[a][:], tab_words[a].rearrange("p t i -> p (t i)").bitcast(I32))
+        bias = keep.tile([M, 1], F32, name="bias")
         identity = keep.tile([P, P], F32, name="identity")
         make_identity(nc, identity[:])
-        bias = keep.tile([M, 1], F32, name="bias")
         nc.sync.dma_start(bias[:], b.rearrange("(n o) -> n o", o=1))
 
         picked_scales = keep.tile([P, S], U8, name="picked_scales")
         nc.vector.tensor_copy(picked_scales[:], scale_table[:].indirect(offsets[:]))
-        for quad in range(4):
+        for quad in MOVE_ORDER:
             nc.sync.dma_start(
-                planes[32 * quad : 32 * quad + 8, :].bitcast(I32), picked_scales[96 + quad : P : 4, :].bitcast(I32)
+                v_scales[QUADRANT * quad : QUADRANT * quad + PASSES * QUAD_ROWS, :].bitcast(I32),
+                picked_scales[FIRST_ROW + quad : P : QUAD_ROWS, :].bitcast(I32),
             )
         residual = keep.tile([P, T], F32, name="residual", tag="scales_then_residual")
         nc.sync.dma_start(residual[:], rT)
@@ -83,34 +88,37 @@ def tile_list_tabres_gelu_kernel(tc, tab_words, tab_scales, w, rT, b, offs, out)
         parts = keep.tile([P, 2 * PASSES * BANK], BF16, name="parts", tag="parts_then_picked1", align_bytes=64)
         for a in range(PASSES):
             lo_sum = psum.tile([P, PACK, M], F32, name="lo_sum%d" % a)
-            hi_back = psum.tile([P, PACK, M], F32, name="hi_back%d" % a, tag="turn%d" % a)
+            minus_hi_back = psum.tile([P, PACK, M], F32, name="minus_hi_back%d" % a, tag="turn%d" % a)
+            blocks = [slice(a * BANK + i * P, a * BANK + (i + 1) * P) for i in range(PACK)]
             for term, source in enumerate((w_turned, minus_hi)):
                 for i in range(PACK):
                     nc.tensor.matmul(
                         lo_sum[:, i, :],
-                        source[:, a * BANK + i * P : a * BANK + (i + 1) * P],
+                        source[:, blocks[i]],
                         identity[:],
                         start=(term == 0 and i == 0),
                         stop=(term == 1 and i == PACK - 1),
                         is_transpose=True,
                     )
             for i in range(PACK):
-                nc.tensor.transpose(hi_back[:, i, :], minus_hi[:, a * BANK + i * P : a * BANK + (i + 1) * P], identity[:])
+                nc.tensor.transpose(minus_hi_back[:, i, :], minus_hi[:, blocks[i]], identity[:])
             hi_cols = parts[:, a * BANK : (a + 1) * BANK].rearrange("p (n i) -> p n i", i=PACK)
             lo_cols = parts[:, (PASSES + a) * BANK : (PASSES + a + 1) * BANK].rearrange("p (n i) -> p n i", i=PACK)
             nc.scalar.copy(lo_cols, lo_sum[:].rearrange("p i n -> p n i"))
-            nc.scalar.activation(hi_cols, hi_back[:].rearrange("p i n -> p n i"), ACT.Copy, scale=-1.0)
+            nc.scalar.activation(hi_cols, minus_hi_back[:].rearrange("p i n -> p n i"), ACT.Copy, scale=-1.0)
 
         picked0 = keep.tile([P, S], U32, name="picked0", tag="w_turned_then_picked0", align_bytes=64)
         nc.vector.tensor_copy(picked0[:], word_tables[0][:].bitcast(U32).indirect(offsets[:]))
-        w_codes = keep.tile([P, 2 * PASSES * M], U32, name="w_codes", tag="word_table0", align_bytes=64)
+        w_codes = keep.tile([P, 2 * PASSES * M], U32, name="w_codes", align_bytes=64)
         w_scales = keep.tile([P, 2 * PASSES * M], U8, name="w_scales", align_bytes=64)
         nc.vector.quantize_mx(out=w_codes[:].bitcast(FP8X4), scales=w_scales[:], in_=parts[:])
 
         picked1 = keep.tile([P, S], U32, name="picked1", tag="parts_then_picked1", align_bytes=64)
         activated = []
         for col in range(0, S, BANK):
-            nc.vector.tensor_copy(picked1[:, col : col + BANK], word_tables[1][:].bitcast(U32).indirect(entries(col, BANK)))
+            nc.vector.tensor_copy(
+                picked1[:, col : col + BANK], word_tables[1][:].bitcast(U32).indirect(entries(col, BANK))
+            )
             acc = psum.tile([M, BANK], F32, name="acc%d" % col)
             for a, picked in enumerate((picked0, picked1)):
                 for part in range(2):
@@ -120,7 +128,7 @@ def tile_list_tabres_gelu_kernel(tc, tab_words, tab_scales, w, rT, b, offs, out)
                         lhsT=w_codes[:, w_cols].bitcast(FP8X4),
                         lhsT_scale=w_scales[:, w_cols],
                         rhs=picked[:, col : col + BANK].bitcast(FP8X4),
-                        rhs_scale=planes[4 * a : P, col : col + BANK],
+                        rhs_scale=v_scales[QUAD_ROWS * a : P, col : col + BANK],
                         start=(a == 0 and part == 0),
                         stop=(a == PASSES - 1 and part == 1),
                     )
@@ -128,12 +136,12 @@ def tile_list_tabres_gelu_kernel(tc, tab_words, tab_scales, w, rT, b, offs, out)
             nc.scalar.activation(gelu[:], acc[:], ACT.Gelu_apprx_tanh, bias=bias[:])
             activated.append(gelu)
 
-        lo = 0
+        col = 0
         for width in OUT_WIDTHS:
-            c, inner = divmod(lo, BANK)
-            result = keep.tile([M, width], F32, name="result%d" % lo)
+            bank, inner = divmod(col, BANK)
+            result = keep.tile([M, width], F32, name="result%d" % col)
             nc.vector.tensor_tensor(
-                result[:], residual[:].indirect(entries(lo, width)), activated[c][:, inner : inner + width], ALU.add
+                result[:], residual[:].indirect(entries(col, width)), activated[bank][:, inner : inner + width], ALU.add
             )
-            nc.sync.dma_start(out[:, lo : lo + width], result[:])
-            lo = lo + width
+            nc.sync.dma_start(out[:, col : col + width], result[:])
+            col = col + width

@@ -28,8 +28,9 @@ PASS_ROWS = 16
 FIRST_ROW = P - PASSES * PASS_ROWS
 HI_MASK = -(1 << 20)
 SIGN_BIT = -(1 << 31)
-MOVE_ORDER = (0, 2, 1, 3)
-OUT_WIDTHS = (512, 512, 512, 256, 256)
+EARLY_MOVES = ((0, 0), (1, 0), (0, 1), (1, 1), (0, 2), (0, 3))
+LATE_MOVES = ((1, 2), (1, 3))
+OUT_WIDTHS = (512, 512, 512, 384, 128)
 
 
 def tile_list_tabres_gelu_kernel(tc, tab_words, tab_scales, w, rT, b, offs, out):
@@ -45,35 +46,39 @@ def tile_list_tabres_gelu_kernel(tc, tab_words, tab_scales, w, rT, b, offs, out)
             return offsets[:, first // GROUP : (first + count) // GROUP]
 
         scale_table = keep.tile([P, T], U8, name="scale_table", tag="scales_then_residual")
-        for a in range(PASSES):
-            first = FIRST_ROW + PASS_ROWS * a
-            nc.sync.dma_start(
-                scale_table[first : first + PASS_ROWS, :].bitcast(I32),
-                tab_scales[a].bitcast(I32).rearrange("(q r) t -> r q t", r=QUAD_ROWS),
-            )
+        nc.sync.dma_start(scale_table[FIRST_ROW:P, :].bitcast(I32), tab_scales.bitcast(I32).rearrange("a q t -> (a q) t"))
         nc.vector.memset(scale_table[0:FIRST_ROW, :].bitcast(I32), 0)
-        v_scales = keep.tile([P, S], U8, name="v_scales", align_bytes=64)
-        nc.vector.memset(v_scales[:].bitcast(I32), 0)
+        v_scales = [keep.tile([P, S], U8, name="v_scales%d" % a, align_bytes=64) for a in range(PASSES)]
+        for a in range(PASSES):
+            nc.vector.memset(v_scales[a][:].bitcast(I32), 0)
 
         word_tables = [keep.tile([P, T], I32, name="word_table%d" % a) for a in range(PASSES)]
         w_raw = keep.tile([P, PASSES, PACK, M], F32, name="w_raw")
         nc.sync.dma_start(w_raw[:], w.rearrange("(a p i) n -> p a i n", a=PASSES, i=PACK))
-        for a in range(PASSES):
-            nc.sync.dma_start(word_tables[a][:], tab_words[a].rearrange("p t i -> p (t i)").bitcast(I32))
         bias = keep.tile([M, 1], F32, name="bias")
+        nc.sync.dma_start(word_tables[0][:], tab_words[0].rearrange("p t i -> p (t i)").bitcast(I32))
+        nc.sync.dma_start(bias[:], b.rearrange("(n o) -> n o", o=1))
+        nc.sync.dma_start(word_tables[1][:], tab_words[1].rearrange("p t i -> p (t i)").bitcast(I32))
         identity = keep.tile([P, P], F32, name="identity")
         make_identity(nc, identity[:])
-        nc.sync.dma_start(bias[:], b.rearrange("(n o) -> n o", o=1))
 
         picked_scales = keep.tile([P, S], U8, name="picked_scales")
         nc.vector.tensor_copy(picked_scales[:], scale_table[:].indirect(offsets[:]))
-        for quad in MOVE_ORDER:
+
+        def move_scales(a, r):
+            first = FIRST_ROW + PASS_ROWS * a + r
             nc.sync.dma_start(
-                v_scales[QUADRANT * quad : QUADRANT * quad + PASSES * QUAD_ROWS, :].bitcast(I32),
-                picked_scales[FIRST_ROW + quad : P : QUAD_ROWS, :].bitcast(I32),
+                v_scales[a][QUAD_ROWS * a + r : P : QUADRANT, :].bitcast(I32),
+                picked_scales[first : first + PASS_ROWS - r : QUAD_ROWS, :].bitcast(I32),
             )
+
         residual = keep.tile([P, T], F32, name="residual", tag="scales_then_residual")
-        nc.sync.dma_start(residual[:], rT)
+        for a, r in EARLY_MOVES:
+            move_scales(a, r)
+        nc.sync.dma_start(residual[:, 0 : T // 2], rT[:, 0 : T // 2])
+        for a, r in LATE_MOVES:
+            move_scales(a, r)
+        nc.sync.dma_start(residual[:, T // 2 : T], rT[:, T // 2 : T])
 
         w_turned = keep.tile([M, PASSES * BANK], F32, name="w_turned", tag="w_turned_then_picked0", align_bytes=64)
         for a in range(PASSES):
@@ -86,20 +91,26 @@ def tile_list_tabres_gelu_kernel(tc, tab_words, tab_scales, w, rT, b, offs, out)
             minus_hi[:].bitcast(I32), w_turned[:].bitcast(I32), HI_MASK, SIGN_BIT, ALU.bitwise_and, ALU.bitwise_xor
         )
         parts = keep.tile([P, 2 * PASSES * BANK], BF16, name="parts", tag="parts_then_picked1", align_bytes=64)
+        lo_sums = [psum.tile([P, PACK, M], F32, name="lo_sum%d" % a) for a in range(PASSES)]
+
+        def add_turned(source, a, first_term):
+            for i in range(PACK):
+                nc.tensor.matmul(
+                    lo_sums[a][:, i, :],
+                    source[:, a * BANK + i * P : a * BANK + (i + 1) * P],
+                    identity[:],
+                    start=(first_term and i == 0),
+                    stop=(not first_term and i == PACK - 1),
+                    is_transpose=True,
+                )
+
         for a in range(PASSES):
-            lo_sum = psum.tile([P, PACK, M], F32, name="lo_sum%d" % a)
+            add_turned(w_turned, a, True)
+        for a in range(PASSES):
+            lo_sum = lo_sums[a]
+            add_turned(minus_hi, a, False)
             minus_hi_back = psum.tile([P, PACK, M], F32, name="minus_hi_back%d" % a, tag="turn%d" % a)
             blocks = [slice(a * BANK + i * P, a * BANK + (i + 1) * P) for i in range(PACK)]
-            for term, source in enumerate((w_turned, minus_hi)):
-                for i in range(PACK):
-                    nc.tensor.matmul(
-                        lo_sum[:, i, :],
-                        source[:, blocks[i]],
-                        identity[:],
-                        start=(term == 0 and i == 0),
-                        stop=(term == 1 and i == PACK - 1),
-                        is_transpose=True,
-                    )
             for i in range(PACK):
                 nc.tensor.transpose(minus_hi_back[:, i, :], minus_hi[:, blocks[i]], identity[:])
             hi_cols = parts[:, a * BANK : (a + 1) * BANK].rearrange("p (n i) -> p n i", i=PACK)
@@ -114,24 +125,27 @@ def tile_list_tabres_gelu_kernel(tc, tab_words, tab_scales, w, rT, b, offs, out)
         nc.vector.quantize_mx(out=w_codes[:].bitcast(FP8X4), scales=w_scales[:], in_=parts[:])
 
         picked1 = keep.tile([P, S], U32, name="picked1", tag="parts_then_picked1", align_bytes=64)
+        def multiply(acc, a, picked, col):
+            for part in range(2):
+                w_cols = slice((part * PASSES + a) * M, (part * PASSES + a + 1) * M)
+                nc.tensor.matmul_mx(
+                    out=acc[:],
+                    lhsT=w_codes[:, w_cols].bitcast(FP8X4),
+                    lhsT_scale=w_scales[:, w_cols],
+                    rhs=picked[:, col : col + BANK].bitcast(FP8X4),
+                    rhs_scale=v_scales[a][QUAD_ROWS * a : P, col : col + BANK],
+                    start=(a == 0 and part == 0),
+                    stop=(a == PASSES - 1 and part == 1),
+                )
+
         activated = []
         for col in range(0, S, BANK):
             nc.vector.tensor_copy(
                 picked1[:, col : col + BANK], word_tables[1][:].bitcast(U32).indirect(entries(col, BANK))
             )
-            acc = psum.tile([M, BANK], F32, name="acc%d" % col)
-            for a, picked in enumerate((picked0, picked1)):
-                for part in range(2):
-                    w_cols = slice((part * PASSES + a) * M, (part * PASSES + a + 1) * M)
-                    nc.tensor.matmul_mx(
-                        out=acc[:],
-                        lhsT=w_codes[:, w_cols].bitcast(FP8X4),
-                        lhsT_scale=w_scales[:, w_cols],
-                        rhs=picked[:, col : col + BANK].bitcast(FP8X4),
-                        rhs_scale=v_scales[QUAD_ROWS * a : P, col : col + BANK],
-                        start=(a == 0 and part == 0),
-                        stop=(a == PASSES - 1 and part == 1),
-                    )
+            acc = psum.tile([M, BANK], F32, name="acc", bufs=2)
+            multiply(acc, 0, picked0, col)
+            multiply(acc, 1, picked1, col)
             gelu = keep.tile([M, BANK], F32, name="gelu%d" % col)
             nc.scalar.activation(gelu[:], acc[:], ACT.Gelu_apprx_tanh, bias=bias[:])
             activated.append(gelu)

@@ -54,10 +54,12 @@ def tile_list_tabres_gelu_kernel(tc, tab_words, tab_scales, w, rT, b, offs, out)
 
         word_tables = [keep.tile([P, T], I32, name="word_table%d" % a) for a in range(PASSES)]
         w_raw = keep.tile([P, PASSES, PACK, M], F32, name="w_raw")
+        bias_row = keep.tile([P, M], F32, name="bias_row")
+        nc.gpsimd.memset(bias_row[0 : P - 1, :], 0.0)
+        nc.sync.dma_start(bias_row[P - 1 : P, :], b.rearrange("(o n) -> o n", o=1))
         nc.sync.dma_start(w_raw[:], w.rearrange("(a p i) n -> p a i n", a=PASSES, i=PACK))
         bias = keep.tile([M, 1], F32, name="bias")
         nc.sync.dma_start(word_tables[0][:], tab_words[0].rearrange("p t i -> p (t i)").bitcast(I32))
-        nc.sync.dma_start(bias[:], b.rearrange("(n o) -> n o", o=1))
         nc.sync.dma_start(word_tables[1][:], tab_words[1].rearrange("p t i -> p (t i)").bitcast(I32))
         identity = keep.tile([P, P], F32, name="identity")
         make_identity(nc, identity[:])
@@ -117,6 +119,10 @@ def tile_list_tabres_gelu_kernel(tc, tab_words, tab_scales, w, rT, b, offs, out)
             lo_cols = parts[:, (PASSES + a) * BANK : (PASSES + a + 1) * BANK].rearrange("p (n i) -> p n i", i=PACK)
             nc.scalar.copy(lo_cols, lo_sum[:].rearrange("p i n -> p n i"))
             nc.scalar.activation(hi_cols, minus_hi_back[:].rearrange("p i n -> p n i"), ACT.Copy, scale=-1.0)
+
+        bias_turned = psum.tile([M, P], F32, name="bias_turned")
+        nc.tensor.transpose(bias_turned[:], bias_row[:], identity[:])
+        nc.scalar.copy(bias[:], bias_turned[:, P - 1 : P])
 
         picked0 = keep.tile([P, S], U32, name="picked0", tag="w_turned_then_picked0", align_bytes=64)
         nc.vector.tensor_copy(picked0[:], word_tables[0][:].bitcast(U32).indirect(offsets[:]))

@@ -50,7 +50,7 @@ def tile_list_tabres_gelu_kernel(tc, tab_words, tab_scales, w, rT, b, offs, out)
         nc.vector.memset(scale_table[0:FIRST_ROW, :].bitcast(I32), 0)
         v_scales = [keep.tile([P, S], U8, name="v_scales%d" % a, align_bytes=64) for a in range(PASSES)]
         for a in range(PASSES):
-            nc.vector.memset(v_scales[a][:].bitcast(I32), 0)
+            nc.gpsimd.memset(v_scales[a][:].bitcast(I32), 0)
 
         word_tables = [keep.tile([P, T], I32, name="word_table%d" % a) for a in range(PASSES)]
         w_raw = keep.tile([P, PASSES, PACK, M], F32, name="w_raw")
@@ -82,58 +82,50 @@ def tile_list_tabres_gelu_kernel(tc, tab_words, tab_scales, w, rT, b, offs, out)
             move_scales(a, r)
         nc.sync.dma_start(residual[:, T // 2 : T], rT[:, T // 2 : T])
 
-        w_turned = keep.tile([M, PASSES * BANK], F32, name="w_turned", tag="w_turned_then_picked0", align_bytes=64)
-        for a in range(PASSES):
-            turned = psum.tile([M, PACK, P], F32, name="turned%d" % a, tag="turn%d" % a)
-            for i in range(PACK):
-                nc.tensor.transpose(turned[:, i, :], w_raw[:, a, i, :], identity[:])
-            nc.scalar.copy(w_turned[:, a * BANK : (a + 1) * BANK], turned[:].rearrange("n i p -> n (i p)"))
-        minus_hi = keep.tile([M, PASSES * BANK], F32, name="minus_hi")
-        nc.vector.tensor_scalar(
-            minus_hi[:].bitcast(I32), w_turned[:].bitcast(I32), HI_MASK, SIGN_BIT, ALU.bitwise_and, ALU.bitwise_xor
-        )
-        parts = keep.tile([P, 2 * PASSES * BANK], BF16, name="parts", tag="parts_then_picked1", align_bytes=64)
-        lo_sums = [psum.tile([P, PACK, M], F32, name="lo_sum%d" % a) for a in range(PASSES)]
-
-        def add_turned(source, a, first_term):
-            for i in range(PACK):
-                nc.tensor.matmul(
-                    lo_sums[a][:, i, :],
-                    source[:, a * BANK + i * P : a * BANK + (i + 1) * P],
-                    identity[:],
-                    start=(first_term and i == 0),
-                    stop=(not first_term and i == PACK - 1),
-                    is_transpose=True,
-                )
-
-        for a in range(PASSES):
-            add_turned(w_turned, a, True)
-        for a in range(PASSES):
-            lo_sum = lo_sums[a]
-            add_turned(minus_hi, a, False)
-            minus_hi_back = psum.tile([P, PACK, M], F32, name="minus_hi_back%d" % a, tag="turn%d" % a)
-            blocks = [slice(a * BANK + i * P, a * BANK + (i + 1) * P) for i in range(PACK)]
-            for i in range(PACK):
-                nc.tensor.transpose(minus_hi_back[:, i, :], minus_hi[:, blocks[i]], identity[:])
-            hi_cols = parts[:, a * BANK : (a + 1) * BANK].rearrange("p (n i) -> p n i", i=PACK)
-            lo_cols = parts[:, (PASSES + a) * BANK : (PASSES + a + 1) * BANK].rearrange("p (n i) -> p n i", i=PACK)
-            nc.scalar.copy(lo_cols, lo_sum[:].rearrange("p i n -> p n i"))
-            nc.scalar.activation(hi_cols, minus_hi_back[:].rearrange("p i n -> p n i"), ACT.Copy, scale=-1.0)
-
         bias_turned = psum.tile([M, P], F32, name="bias_turned")
         nc.tensor.transpose(bias_turned[:], bias_row[:], identity[:])
         nc.scalar.copy(bias[:], bias_turned[:, P - 1 : P])
-
-        picked0 = keep.tile([P, S], U32, name="picked0", tag="w_turned_then_picked0", align_bytes=64)
+        minus_hi = keep.tile([P, PASSES, PACK, M], F32, name="minus_hi", tag="minus_hi_then_picked1", align_bytes=64)
+        nc.vector.tensor_scalar(
+            minus_hi[:].bitcast(I32), w_raw[:].bitcast(I32), HI_MASK, SIGN_BIT, ALU.bitwise_and, ALU.bitwise_xor
+        )
+        picked0 = keep.tile([P, S], U32, name="picked0", align_bytes=64)
         nc.vector.tensor_copy(picked0[:], word_tables[0][:].bitcast(U32).indirect(offsets[:]))
+
+        lo_sums = [psum.tile([M, PACK, P], F32, name="lo_sum%d" % a) for a in range(PASSES)]
+        for term, source in enumerate((w_raw, minus_hi)):
+            for a in range(PASSES):
+                for i in range(PACK):
+                    nc.tensor.matmul(
+                        lo_sums[a][:, i, :],
+                        source[:, a, i, :],
+                        identity[:],
+                        start=(term == 0 and i == 0),
+                        stop=(term == 1 and i == PACK - 1),
+                        is_transpose=True,
+                    )
         w_codes = keep.tile([P, 2 * PASSES * M], U32, name="w_codes", align_bytes=64)
         w_scales = keep.tile([P, 2 * PASSES * M], U8, name="w_scales", align_bytes=64)
-        nc.vector.quantize_mx(out=w_codes[:].bitcast(FP8X4), scales=w_scales[:], in_=parts[:])
+        for a in range(PASSES):
+            lo_turned = keep.tile([M, PACK, P], F32, name="lo_turned%d" % a, tag="lo_turned%d" % a, align_bytes=64)
+            nc.scalar.copy(lo_turned[:], lo_sums[a][:])
+            lo_back = psum.tile([P, PACK, M], F32, name="lo_back%d" % a)
+            for i in range(PACK):
+                nc.tensor.transpose(lo_back[:, i, :], lo_turned[:, i, :], identity[:])
+            tag = "lo_turned%d" % a if a == PASSES - 1 else "parts%d" % a
+            parts = keep.tile([P, 2, M, PACK], BF16, name="parts%d" % a, tag=tag, align_bytes=64)
+            nc.scalar.copy(parts[:, 1, :, :], lo_back[:].rearrange("p i n -> p n i"))
+            nc.scalar.activation(parts[:, 0, :, :], minus_hi[:, a, :, :].rearrange("p i n -> p n i"), ACT.Copy, scale=-1.0)
+            cols = slice(2 * a * M, 2 * (a + 1) * M)
+            nc.vector.quantize_mx(
+                out=w_codes[:, cols].bitcast(FP8X4), scales=w_scales[:, cols], in_=parts[:].rearrange("p h n i -> p (h n i)")
+            )
 
-        picked1 = keep.tile([P, S], U32, name="picked1", tag="parts_then_picked1", align_bytes=64)
+        picked1 = keep.tile([P, S], U32, name="picked1", tag="minus_hi_then_picked1", align_bytes=64)
+
         def multiply(acc, a, picked, col):
             for part in range(2):
-                w_cols = slice((part * PASSES + a) * M, (part * PASSES + a + 1) * M)
+                w_cols = slice((2 * a + part) * M, (2 * a + part + 1) * M)
                 nc.tensor.matmul_mx(
                     out=acc[:],
                     lhsT=w_codes[:, w_cols].bitcast(FP8X4),

@@ -20,6 +20,7 @@ ACT = mybir.ActivationFunctionType
 P = 128
 PACK = 4
 PASSES = K // (P * PACK)
+PARTS = 2
 BANK = 512
 GROUP = 16
 QUADRANT = 32
@@ -28,8 +29,10 @@ PASS_ROWS = 16
 FIRST_ROW = P - PASSES * PASS_ROWS
 HI_MASK = -(1 << 20)
 SIGN_BIT = -(1 << 31)
-EARLY_MOVES = ((0, 0), (1, 0), (0, 1), (1, 1), (0, 2), (0, 3))
-LATE_MOVES = ((1, 2), (1, 3))
+MOVES_AHEAD_OF_RT = ((0, 0), (1, 0), (0, 1), (1, 1), (0, 2), (0, 3))
+MOVES_INSIDE_RT = ((1, 2), (1, 3))
+RT_SPLIT = 3 * T // 8
+SUM_BANKS = 2
 OUT_WIDTHS = (512, 512, 512, 384, 128)
 
 
@@ -59,8 +62,8 @@ def tile_list_tabres_gelu_kernel(tc, tab_words, tab_scales, w, rT, b, offs, out)
         nc.sync.dma_start(bias_row[P - 1 : P, :], b.rearrange("(o n) -> o n", o=1))
         nc.sync.dma_start(w_raw[:], w.rearrange("(a p i) n -> p a i n", a=PASSES, i=PACK))
         bias = keep.tile([M, 1], F32, name="bias")
-        nc.sync.dma_start(word_tables[0][:], tab_words[0].rearrange("p t i -> p (t i)").bitcast(I32))
-        nc.sync.dma_start(word_tables[1][:], tab_words[1].rearrange("p t i -> p (t i)").bitcast(I32))
+        for a in range(PASSES):
+            nc.sync.dma_start(word_tables[a][:], tab_words[a].rearrange("p t i -> p (t i)").bitcast(I32))
         identity = keep.tile([P, P], F32, name="identity")
         make_identity(nc, identity[:])
 
@@ -68,23 +71,24 @@ def tile_list_tabres_gelu_kernel(tc, tab_words, tab_scales, w, rT, b, offs, out)
         nc.vector.tensor_copy(picked_scales[:], scale_table[:].indirect(offsets[:]))
 
         def move_scales(a, r):
-            first = FIRST_ROW + PASS_ROWS * a + r
+            pass_first = FIRST_ROW + PASS_ROWS * a
             nc.sync.dma_start(
                 v_scales[a][QUAD_ROWS * a + r : P : QUADRANT, :].bitcast(I32),
-                picked_scales[first : first + PASS_ROWS - r : QUAD_ROWS, :].bitcast(I32),
+                picked_scales[pass_first + r : pass_first + PASS_ROWS : QUAD_ROWS, :].bitcast(I32),
             )
 
         residual = keep.tile([P, T], F32, name="residual", tag="scales_then_residual")
-        for a, r in EARLY_MOVES:
+        for a, r in MOVES_AHEAD_OF_RT:
             move_scales(a, r)
-        nc.sync.dma_start(residual[:, 0 : T // 2], rT[:, 0 : T // 2])
-        for a, r in LATE_MOVES:
+        nc.sync.dma_start(residual[:, 0:RT_SPLIT], rT[:, 0:RT_SPLIT])
+        for a, r in MOVES_INSIDE_RT:
             move_scales(a, r)
-        nc.sync.dma_start(residual[:, T // 2 : T], rT[:, T // 2 : T])
+        nc.sync.dma_start(residual[:, RT_SPLIT:T], rT[:, RT_SPLIT:T])
 
         bias_turned = psum.tile([M, P], F32, name="bias_turned")
         nc.tensor.transpose(bias_turned[:], bias_row[:], identity[:])
         nc.scalar.copy(bias[:], bias_turned[:, P - 1 : P])
+
         minus_hi = keep.tile([P, PASSES, PACK, M], F32, name="minus_hi", tag="minus_hi_then_picked1", align_bytes=64)
         nc.vector.tensor_scalar(
             minus_hi[:].bitcast(I32), w_raw[:].bitcast(I32), HI_MASK, SIGN_BIT, ALU.bitwise_and, ALU.bitwise_xor
@@ -104,28 +108,30 @@ def tile_list_tabres_gelu_kernel(tc, tab_words, tab_scales, w, rT, b, offs, out)
                         stop=(term == 1 and i == PACK - 1),
                         is_transpose=True,
                     )
-        w_codes = keep.tile([P, 2 * PASSES * M], U32, name="w_codes", align_bytes=64)
-        w_scales = keep.tile([P, 2 * PASSES * M], U8, name="w_scales", align_bytes=64)
+        w_codes = keep.tile([P, PASSES * PARTS * M], U32, name="w_codes", align_bytes=64)
+        w_scales = keep.tile([P, PASSES * PARTS * M], U8, name="w_scales", align_bytes=64)
         for a in range(PASSES):
             lo_turned = keep.tile([M, PACK, P], F32, name="lo_turned%d" % a, tag="lo_turned%d" % a, align_bytes=64)
             nc.scalar.copy(lo_turned[:], lo_sums[a][:])
             lo_back = psum.tile([P, PACK, M], F32, name="lo_back%d" % a)
             for i in range(PACK):
                 nc.tensor.transpose(lo_back[:, i, :], lo_turned[:, i, :], identity[:])
-            tag = "lo_turned%d" % a if a == PASSES - 1 else "parts%d" % a
-            parts = keep.tile([P, 2, M, PACK], BF16, name="parts%d" % a, tag=tag, align_bytes=64)
+            parts_tag = "lo_turned%d" % a if a == PASSES - 1 else "parts%d" % a
+            parts = keep.tile([P, PARTS, M, PACK], BF16, name="parts%d" % a, tag=parts_tag, align_bytes=64)
             nc.scalar.copy(parts[:, 1, :, :], lo_back[:].rearrange("p i n -> p n i"))
             nc.scalar.activation(parts[:, 0, :, :], minus_hi[:, a, :, :].rearrange("p i n -> p n i"), ACT.Copy, scale=-1.0)
-            cols = slice(2 * a * M, 2 * (a + 1) * M)
+            pass_cols = slice(PARTS * a * M, PARTS * (a + 1) * M)
             nc.vector.quantize_mx(
-                out=w_codes[:, cols].bitcast(FP8X4), scales=w_scales[:, cols], in_=parts[:].rearrange("p h n i -> p (h n i)")
+                out=w_codes[:, pass_cols].bitcast(FP8X4),
+                scales=w_scales[:, pass_cols],
+                in_=parts[:].rearrange("p h n i -> p (h n i)"),
             )
 
         picked1 = keep.tile([P, S], U32, name="picked1", tag="minus_hi_then_picked1", align_bytes=64)
 
         def multiply(acc, a, picked, col):
-            for part in range(2):
-                w_cols = slice((2 * a + part) * M, (2 * a + part + 1) * M)
+            for part in range(PARTS):
+                w_cols = slice((PARTS * a + part) * M, (PARTS * a + part + 1) * M)
                 nc.tensor.matmul_mx(
                     out=acc[:],
                     lhsT=w_codes[:, w_cols].bitcast(FP8X4),
@@ -133,7 +139,7 @@ def tile_list_tabres_gelu_kernel(tc, tab_words, tab_scales, w, rT, b, offs, out)
                     rhs=picked[:, col : col + BANK].bitcast(FP8X4),
                     rhs_scale=v_scales[a][QUAD_ROWS * a : P, col : col + BANK],
                     start=(a == 0 and part == 0),
-                    stop=(a == PASSES - 1 and part == 1),
+                    stop=(a == PASSES - 1 and part == PARTS - 1),
                 )
 
         activated = []
@@ -141,7 +147,7 @@ def tile_list_tabres_gelu_kernel(tc, tab_words, tab_scales, w, rT, b, offs, out)
             nc.vector.tensor_copy(
                 picked1[:, col : col + BANK], word_tables[1][:].bitcast(U32).indirect(entries(col, BANK))
             )
-            acc = psum.tile([M, BANK], F32, name="acc", bufs=2)
+            acc = psum.tile([M, BANK], F32, name="acc", bufs=SUM_BANKS)
             multiply(acc, 0, picked0, col)
             multiply(acc, 1, picked1, col)
             gelu = keep.tile([M, BANK], F32, name="gelu%d" % col)

@@ -27,8 +27,10 @@ QUADRANT = 32
 QUAD_ROWS = 4
 PASS_ROWS = 16
 FIRST_ROW = P - PASSES * PASS_ROWS
-HI_MASK = -(1 << 20)
-SIGN_BIT = -(1 << 31)
+KEPT_BIT = float(1 << 20)
+FLOOR_SHIFT = -15.0 / 32.0
+RUNS = 2
+KIB = 1024
 MOVES_AHEAD_OF_RT = ((0, 0), (1, 0), (0, 1), (1, 1), (0, 2), (0, 3))
 MOVES_INSIDE_RT = ((1, 2), (1, 3))
 RT_SPLIT = 3 * T // 8
@@ -40,6 +42,7 @@ def tile_list_tabres_gelu_kernel(tc, tab_words, tab_scales, w, rT, b, offs, out)
     nc = tc.nc
     with ExitStack() as ctx:
         keep = ctx.enter_context(tc.tile_pool(name="keep", bufs=1))
+        shared = ctx.enter_context(tc.tile_pool(name="shared", bufs=1))
         psum = ctx.enter_context(tc.psum_pool(name="psum", bufs=1))
 
         offsets = keep.tile([P, S // GROUP], U16, name="offsets")
@@ -49,23 +52,26 @@ def tile_list_tabres_gelu_kernel(tc, tab_words, tab_scales, w, rT, b, offs, out)
             return offsets[:, first // GROUP : (first + count) // GROUP]
 
         scale_table = keep.tile([P, T], U8, name="scale_table", tag="scales_then_residual")
-        nc.sync.dma_start(scale_table[FIRST_ROW:P, :].bitcast(I32), tab_scales.bitcast(I32).rearrange("a q t -> (a q) t"))
+        nc.scalar.dma_start(scale_table[FIRST_ROW:P, :].bitcast(I32), tab_scales.bitcast(I32).rearrange("a q t -> (a q) t"))
         nc.vector.memset(scale_table[0:FIRST_ROW, :].bitcast(I32), 0)
+        bias_row = keep.tile([P, M], F32, name="bias_row")
+        nc.gpsimd.memset(bias_row[0 : P - 1, :], 0.0)
+        nc.scalar.dma_start(bias_row[P - 1 : P, :], b.rearrange("(o n) -> o n", o=1))
+        w_raw = [keep.tile([P, PACK, M], F32, name="w_raw%d" % a) for a in range(PASSES)]
+        word_tables = [keep.tile([P, T], I32, name="word_table%d" % a) for a in range(PASSES)]
+        for a in range(PASSES):
+            nc.sync.dma_start(w_raw[a][:], w.rearrange("(a p i) n -> a p i n", a=PASSES, i=PACK)[a])
+            nc.sync.dma_start(word_tables[a][:], tab_words[a].rearrange("p t i -> p (t i)").bitcast(I32))
+
+        identity = keep.tile([P, P], F32, name="identity")
+        make_identity(nc, identity[:])
         v_scales = [keep.tile([P, S], U8, name="v_scales%d" % a, align_bytes=64) for a in range(PASSES)]
         for a in range(PASSES):
             nc.gpsimd.memset(v_scales[a][:].bitcast(I32), 0)
-
-        word_tables = [keep.tile([P, T], I32, name="word_table%d" % a) for a in range(PASSES)]
-        w_raw = keep.tile([P, PASSES, PACK, M], F32, name="w_raw")
-        bias_row = keep.tile([P, M], F32, name="bias_row")
-        nc.gpsimd.memset(bias_row[0 : P - 1, :], 0.0)
-        nc.sync.dma_start(bias_row[P - 1 : P, :], b.rearrange("(o n) -> o n", o=1))
-        nc.sync.dma_start(w_raw[:], w.rearrange("(a p i) n -> p a i n", a=PASSES, i=PACK))
+        bias_turned = psum.tile([M, P], F32, name="bias_turned")
+        nc.tensor.transpose(bias_turned[:], bias_row[:], identity[:])
         bias = keep.tile([M, 1], F32, name="bias")
-        for a in range(PASSES):
-            nc.sync.dma_start(word_tables[a][:], tab_words[a].rearrange("p t i -> p (t i)").bitcast(I32))
-        identity = keep.tile([P, P], F32, name="identity")
-        make_identity(nc, identity[:])
+        nc.scalar.copy(bias[:], bias_turned[:, P - 1 : P])
 
         picked_scales = keep.tile([P, S], U8, name="picked_scales")
         nc.vector.tensor_copy(picked_scales[:], scale_table[:].indirect(offsets[:]))
@@ -85,71 +91,62 @@ def tile_list_tabres_gelu_kernel(tc, tab_words, tab_scales, w, rT, b, offs, out)
             move_scales(a, r)
         nc.sync.dma_start(residual[:, RT_SPLIT:T], rT[:, RT_SPLIT:T])
 
-        bias_turned = psum.tile([M, P], F32, name="bias_turned")
-        nc.tensor.transpose(bias_turned[:], bias_row[:], identity[:])
-        nc.scalar.copy(bias[:], bias_turned[:, P - 1 : P])
-
-        minus_hi = keep.tile([P, PASSES, PACK, M], F32, name="minus_hi", tag="minus_hi_then_picked1", align_bytes=64)
-        nc.vector.tensor_scalar(
-            minus_hi[:].bitcast(I32), w_raw[:].bitcast(I32), HI_MASK, SIGN_BIT, ALU.bitwise_and, ALU.bitwise_xor
-        )
-        picked0 = keep.tile([P, S], U32, name="picked0", align_bytes=64)
-        nc.vector.tensor_copy(picked0[:], word_tables[0][:].bitcast(U32).indirect(offsets[:]))
-
-        lo_sums = [psum.tile([M, PACK, P], F32, name="lo_sum%d" % a) for a in range(PASSES)]
-        for term, source in enumerate((w_raw, minus_hi)):
-            for a in range(PASSES):
-                for i in range(PACK):
-                    nc.tensor.matmul(
-                        lo_sums[a][:, i, :],
-                        source[:, a, i, :],
-                        identity[:],
-                        start=(term == 0 and i == 0),
-                        stop=(term == 1 and i == PACK - 1),
-                        is_transpose=True,
-                    )
         w_codes = keep.tile([P, PASSES * PARTS * M], U32, name="w_codes", align_bytes=64)
         w_scales = keep.tile([P, PASSES * PARTS * M], U8, name="w_scales", align_bytes=64)
+        upper_at = (0, 3 * KIB)
+        hi_at = (4 * KIB, 13 * KIB)
+        picked_at = (5 * KIB, 13 * KIB)
+        picked = []
+        runs = [slice(h * M // RUNS, (h + 1) * M // RUNS) for h in range(RUNS)]
         for a in range(PASSES):
-            lo_turned = keep.tile([M, PACK, P], F32, name="lo_turned%d" % a, tag="lo_turned%d" % a, align_bytes=64)
-            nc.scalar.copy(lo_turned[:], lo_sums[a][:])
-            lo_back = psum.tile([P, PACK, M], F32, name="lo_back%d" % a)
-            for i in range(PACK):
-                nc.tensor.transpose(lo_back[:, i, :], lo_turned[:, i, :], identity[:])
-            parts_tag = "lo_turned%d" % a if a == PASSES - 1 else "parts%d" % a
-            parts = keep.tile([P, PARTS, M, PACK], BF16, name="parts%d" % a, tag=parts_tag, align_bytes=64)
-            nc.scalar.copy(parts[:, 1, :, :], lo_back[:].rearrange("p i n -> p n i"))
-            nc.scalar.activation(parts[:, 0, :, :], minus_hi[:, a, :, :].rearrange("p i n -> p n i"), ACT.Copy, scale=-1.0)
+            upper = shared.tile([P, PACK, M], F32, name="upper%d" % a, offset=upper_at[a], align_bytes=64)
+            kept = keep.tile([P, PACK, M], U32, name="kept%d" % a)
+            hi = shared.tile([P, PACK, M], F32, name="hi%d" % a, offset=hi_at[a], align_bytes=64)
+            parts = keep.tile([P, PARTS, M, PACK], BF16, name="parts%d" % a, align_bytes=64)
+            halves = w_raw[a][:].bitcast(BF16)
+            for run in runs:
+                nc.scalar.activation(upper[:, :, run], halves[:, :, 2 * run.start + 1 : 2 * run.stop : 2], ACT.Copy)
+            for run in runs:
+                nc.scalar.activation(
+                    kept[:, :, run], upper[:, :, run].bitcast(U32), ACT.Copy, scale=1.0 / KEPT_BIT, bias=FLOOR_SHIFT
+                )
+            for run in runs:
+                nc.scalar.activation(hi[:, :, run].bitcast(U32), kept[:, :, run], ACT.Copy, scale=KEPT_BIT)
+            for run in runs:
+                hi_run = hi[:, :, run].rearrange("p i n -> p n i")
+                nc.gpsimd.tensor_tensor(
+                    parts[:, 1, run, :], w_raw[a][:, :, run].rearrange("p i n -> p n i"), hi_run, ALU.subtract
+                )
+                nc.scalar.copy(parts[:, 0, run, :], hi_run)
             pass_cols = slice(PARTS * a * M, PARTS * (a + 1) * M)
             nc.vector.quantize_mx(
                 out=w_codes[:, pass_cols].bitcast(FP8X4),
                 scales=w_scales[:, pass_cols],
                 in_=parts[:].rearrange("p h n i -> p (h n i)"),
             )
-
-        picked1 = keep.tile([P, S], U32, name="picked1", tag="minus_hi_then_picked1", align_bytes=64)
-
-        def multiply(acc, a, picked, col):
-            for part in range(PARTS):
-                w_cols = slice((PARTS * a + part) * M, (PARTS * a + part + 1) * M)
-                nc.tensor.matmul_mx(
-                    out=acc[:],
-                    lhsT=w_codes[:, w_cols].bitcast(FP8X4),
-                    lhsT_scale=w_scales[:, w_cols],
-                    rhs=picked[:, col : col + BANK].bitcast(FP8X4),
-                    rhs_scale=v_scales[a][QUAD_ROWS * a : P, col : col + BANK],
-                    start=(a == 0 and part == 0),
-                    stop=(a == PASSES - 1 and part == PARTS - 1),
+            words = shared.tile([P, S], U32, name="picked%d" % a, offset=picked_at[a], align_bytes=64)
+            width = S // (a + 1)
+            for col in range(0, S, width):
+                nc.vector.tensor_copy(
+                    words[:, col : col + width], word_tables[a][:].bitcast(U32).indirect(entries(col, width))
                 )
+            picked.append(words)
 
         activated = []
         for col in range(0, S, BANK):
-            nc.vector.tensor_copy(
-                picked1[:, col : col + BANK], word_tables[1][:].bitcast(U32).indirect(entries(col, BANK))
-            )
             acc = psum.tile([M, BANK], F32, name="acc", bufs=SUM_BANKS)
-            multiply(acc, 0, picked0, col)
-            multiply(acc, 1, picked1, col)
+            for a in range(PASSES):
+                for part in range(PARTS):
+                    w_cols = slice((PARTS * a + part) * M, (PARTS * a + part + 1) * M)
+                    nc.tensor.matmul_mx(
+                        out=acc[:],
+                        lhsT=w_codes[:, w_cols].bitcast(FP8X4),
+                        lhsT_scale=w_scales[:, w_cols],
+                        rhs=picked[a][:, col : col + BANK].bitcast(FP8X4),
+                        rhs_scale=v_scales[a][QUAD_ROWS * a : P, col : col + BANK],
+                        start=(a == 0 and part == 0),
+                        stop=(a == PASSES - 1 and part == PARTS - 1),
+                    )
             gelu = keep.tile([M, BANK], F32, name="gelu%d" % col)
             nc.scalar.activation(gelu[:], acc[:], ACT.Gelu_apprx_tanh, bias=bias[:])
             activated.append(gelu)

@@ -29,7 +29,8 @@ PASS_ROWS = 16
 FIRST_ROW = P - PASSES * PASS_ROWS
 KEPT_BIT = float(1 << 20)
 FLOOR_SHIFT = -15.0 / 32.0
-RUNS = 2
+RUNS = 4
+LINE = 4
 KIB = 1024
 MOVES_AHEAD_OF_RT = ((0, 0), (1, 0), (0, 1), (1, 1), (0, 2), (0, 3))
 MOVES_INSIDE_RT = ((1, 2), (1, 3))
@@ -98,6 +99,13 @@ def tile_list_tabres_gelu_kernel(tc, tab_words, tab_scales, w, rT, b, offs, out)
         picked_at = (5 * KIB, 13 * KIB)
         picked = []
         runs = [slice(h * M // RUNS, (h + 1) * M // RUNS) for h in range(RUNS)]
+
+        def by_lines(source):
+            return source.rearrange("p i (c j) -> p c i j", j=LINE)
+
+        def by_lines_out(target):
+            return target.rearrange("p (c j) i -> p c i j", j=LINE)
+
         for a in range(PASSES):
             upper = shared.tile([P, PACK, M], F32, name="upper%d" % a, offset=upper_at[a], align_bytes=64)
             kept = keep.tile([P, PACK, M], U32, name="kept%d" % a)
@@ -106,18 +114,15 @@ def tile_list_tabres_gelu_kernel(tc, tab_words, tab_scales, w, rT, b, offs, out)
             halves = w_raw[a][:].bitcast(BF16)
             for run in runs:
                 nc.scalar.activation(upper[:, :, run], halves[:, :, 2 * run.start + 1 : 2 * run.stop : 2], ACT.Copy)
-            for run in runs:
                 nc.scalar.activation(
                     kept[:, :, run], upper[:, :, run].bitcast(U32), ACT.Copy, scale=1.0 / KEPT_BIT, bias=FLOOR_SHIFT
                 )
-            for run in runs:
                 nc.scalar.activation(hi[:, :, run].bitcast(U32), kept[:, :, run], ACT.Copy, scale=KEPT_BIT)
-            for run in runs:
-                hi_run = hi[:, :, run].rearrange("p i n -> p n i")
                 nc.gpsimd.tensor_tensor(
-                    parts[:, 1, run, :], w_raw[a][:, :, run].rearrange("p i n -> p n i"), hi_run, ALU.subtract
+                    by_lines_out(parts[:, 1, run, :]), by_lines(w_raw[a][:, :, run]), by_lines(hi[:, :, run]), ALU.subtract
                 )
-                nc.scalar.copy(parts[:, 0, run, :], hi_run)
+            for run in runs:
+                nc.scalar.copy(by_lines_out(parts[:, 0, run, :]), by_lines(hi[:, :, run]))
             pass_cols = slice(PARTS * a * M, PARTS * (a + 1) * M)
             nc.vector.quantize_mx(
                 out=w_codes[:, pass_cols].bitcast(FP8X4),

@@ -32,11 +32,16 @@ FLOOR_SHIFT = -15.0 / 32.0
 RUNS = 4
 LINE = 4
 KIB = 1024
+UPPER_AT = (0, 3 * KIB)
+HI_AT = (4 * KIB, 13 * KIB)
+PICKED_AT = (5 * KIB, 13 * KIB)
+GATHER_WIDTHS = (S, S // 2)
 MOVES_AHEAD_OF_RT = ((0, 0), (1, 0), (0, 1), (1, 1), (0, 2), (0, 3))
 MOVES_INSIDE_RT = ((1, 2), (1, 3))
 RT_SPLIT = 3 * T // 8
 SUM_BANKS = 2
 OUT_WIDTHS = (512, 512, 512, 384, 128)
+OUT_STORES = (2, 2, 1, 1, 1)
 
 
 def tile_list_tabres_gelu_kernel(tc, tab_words, tab_scales, w, rT, b, offs, out):
@@ -92,24 +97,20 @@ def tile_list_tabres_gelu_kernel(tc, tab_words, tab_scales, w, rT, b, offs, out)
             move_scales(a, r)
         nc.sync.dma_start(residual[:, RT_SPLIT:T], rT[:, RT_SPLIT:T])
 
-        w_codes = keep.tile([P, PASSES * PARTS * M], U32, name="w_codes", align_bytes=64)
-        w_scales = keep.tile([P, PASSES * PARTS * M], U8, name="w_scales", align_bytes=64)
-        upper_at = (0, 3 * KIB)
-        hi_at = (4 * KIB, 13 * KIB)
-        picked_at = (5 * KIB, 13 * KIB)
-        picked = []
-        runs = [slice(h * M // RUNS, (h + 1) * M // RUNS) for h in range(RUNS)]
-
-        def by_lines(source):
+        def read_by_lines(source):
             return source.rearrange("p i (c j) -> p c i j", j=LINE)
 
-        def by_lines_out(target):
+        def write_by_lines(target):
             return target.rearrange("p (c j) i -> p c i j", j=LINE)
 
+        w_codes = keep.tile([P, PASSES * PARTS * M], U32, name="w_codes", align_bytes=64)
+        w_scales = keep.tile([P, PASSES * PARTS * M], U8, name="w_scales", align_bytes=64)
+        picked = []
+        runs = [slice(h * M // RUNS, (h + 1) * M // RUNS) for h in range(RUNS)]
         for a in range(PASSES):
-            upper = shared.tile([P, PACK, M], F32, name="upper%d" % a, offset=upper_at[a], align_bytes=64)
+            upper = shared.tile([P, PACK, M], F32, name="upper%d" % a, offset=UPPER_AT[a], align_bytes=64)
             kept = keep.tile([P, PACK, M], U32, name="kept%d" % a)
-            hi = shared.tile([P, PACK, M], F32, name="hi%d" % a, offset=hi_at[a], align_bytes=64)
+            hi = shared.tile([P, PACK, M], F32, name="hi%d" % a, offset=HI_AT[a], align_bytes=64)
             parts = keep.tile([P, PARTS, M, PACK], BF16, name="parts%d" % a, align_bytes=64)
             halves = w_raw[a][:].bitcast(BF16)
             for run in runs:
@@ -119,21 +120,24 @@ def tile_list_tabres_gelu_kernel(tc, tab_words, tab_scales, w, rT, b, offs, out)
                 )
                 nc.scalar.activation(hi[:, :, run].bitcast(U32), kept[:, :, run], ACT.Copy, scale=KEPT_BIT)
                 nc.gpsimd.tensor_tensor(
-                    by_lines_out(parts[:, 1, run, :]), by_lines(w_raw[a][:, :, run]), by_lines(hi[:, :, run]), ALU.subtract
+                    write_by_lines(parts[:, 1, run, :]),
+                    read_by_lines(w_raw[a][:, :, run]),
+                    read_by_lines(hi[:, :, run]),
+                    ALU.subtract,
                 )
             for run in runs:
-                nc.scalar.copy(by_lines_out(parts[:, 0, run, :]), by_lines(hi[:, :, run]))
+                nc.scalar.copy(write_by_lines(parts[:, 0, run, :]), read_by_lines(hi[:, :, run]))
             pass_cols = slice(PARTS * a * M, PARTS * (a + 1) * M)
             nc.vector.quantize_mx(
                 out=w_codes[:, pass_cols].bitcast(FP8X4),
                 scales=w_scales[:, pass_cols],
                 in_=parts[:].rearrange("p h n i -> p (h n i)"),
             )
-            words = shared.tile([P, S], U32, name="picked%d" % a, offset=picked_at[a], align_bytes=64)
-            width = S // (a + 1)
-            for col in range(0, S, width):
+            words = shared.tile([P, S], U32, name="picked%d" % a, offset=PICKED_AT[a], align_bytes=64)
+            count = GATHER_WIDTHS[a]
+            for first in range(0, S, count):
                 nc.vector.tensor_copy(
-                    words[:, col : col + width], word_tables[a][:].bitcast(U32).indirect(entries(col, width))
+                    words[:, first : first + count], word_tables[a][:].bitcast(U32).indirect(entries(first, count))
                 )
             picked.append(words)
 
@@ -157,11 +161,13 @@ def tile_list_tabres_gelu_kernel(tc, tab_words, tab_scales, w, rT, b, offs, out)
             activated.append(gelu)
 
         col = 0
-        for width in OUT_WIDTHS:
+        for width, stores in zip(OUT_WIDTHS, OUT_STORES):
             bank, inner = divmod(col, BANK)
             result = keep.tile([M, width], F32, name="result%d" % col)
             nc.vector.tensor_tensor(
                 result[:], residual[:].indirect(entries(col, width)), activated[bank][:, inner : inner + width], ALU.add
             )
-            nc.sync.dma_start(out[:, col : col + width], result[:])
+            step = width // stores
+            for done in range(0, width, step):
+                nc.sync.dma_start(out[:, col + done : col + done + step], result[:, done : done + step])
             col = col + width

@@ -52,13 +52,13 @@ def tile_list_tabres_gelu_kernel(tc, tab_words, tab_scales, w, rT, b, offs, out)
         psum = ctx.enter_context(tc.psum_pool(name="psum", bufs=1))
 
         offsets = keep.tile([P, S // GROUP], U16, name="offsets")
-        nc.sync.dma_start(offsets[:], offs)
 
         def entries(first, count):
             return offsets[:, first // GROUP : (first + count) // GROUP]
 
         scale_table = keep.tile([P, T], U8, name="scale_table", tag="scales_then_residual")
-        nc.scalar.dma_start(scale_table[FIRST_ROW:P, :].bitcast(I32), tab_scales.bitcast(I32).rearrange("a q t -> (a q) t"))
+        nc.sync.dma_start(scale_table[FIRST_ROW:P, :].bitcast(I32), tab_scales.bitcast(I32).rearrange("a q t -> (a q) t"))
+        nc.sync.dma_start(offsets[:], offs)
         nc.vector.memset(scale_table[0:FIRST_ROW, :].bitcast(I32), 0)
         bias_row = keep.tile([P, M], F32, name="bias_row")
         nc.gpsimd.memset(bias_row[0 : P - 1, :], 0.0)

@@ -38,6 +38,7 @@ PICKED_AT = (5 * KIB, 13 * KIB)
 GATHER_WIDTHS = (S, S // 2)
 MOVES_AHEAD_OF_RT = ((0, 0), (1, 0), (0, 1), (1, 1), (0, 2), (0, 3))
 MOVES_INSIDE_RT = ((1, 2), (1, 3))
+PLANES = ((0, S - BANK), (S - BANK, BANK))
 RT_SPLIT = 3 * T // 8
 SUM_BANKS = 2
 OUT_WIDTHS = (512, 512, 512, 384, 128)
@@ -71,9 +72,12 @@ def tile_list_tabres_gelu_kernel(tc, tab_words, tab_scales, w, rT, b, offs, out)
 
         identity = keep.tile([P, P], F32, name="identity")
         make_identity(nc, identity[:])
-        v_scales = [keep.tile([P, S], U8, name="v_scales%d" % a, align_bytes=64) for a in range(PASSES)]
-        for a in range(PASSES):
-            nc.gpsimd.memset(v_scales[a][:].bitcast(I32), 0)
+        v_scales = {}
+        for first, count in PLANES:
+            for a in range(PASSES):
+                plane = keep.tile([P, count], U8, name="v_scales%d_%d" % (a, first), align_bytes=64)
+                nc.gpsimd.memset(plane[:].bitcast(I32), 0)
+                v_scales[a, first] = plane
         bias_turned = psum.tile([M, P], F32, name="bias_turned")
         nc.tensor.transpose(bias_turned[:], bias_row[:], identity[:])
         bias = keep.tile([M, 1], F32, name="bias")
@@ -82,20 +86,24 @@ def tile_list_tabres_gelu_kernel(tc, tab_words, tab_scales, w, rT, b, offs, out)
         picked_scales = keep.tile([P, S], U8, name="picked_scales")
         nc.vector.tensor_copy(picked_scales[:], scale_table[:].indirect(offsets[:]))
 
-        def move_scales(a, r):
+        def move_scales(a, r, columns):
+            first, count = columns
             pass_first = FIRST_ROW + PASS_ROWS * a
             nc.sync.dma_start(
-                v_scales[a][QUAD_ROWS * a + r : P : QUADRANT, :].bitcast(I32),
-                picked_scales[pass_first + r : pass_first + PASS_ROWS : QUAD_ROWS, :].bitcast(I32),
+                v_scales[a, first][QUAD_ROWS * a + r : P : QUADRANT, :].bitcast(I32),
+                picked_scales[pass_first + r : pass_first + PASS_ROWS : QUAD_ROWS, first : first + count].bitcast(I32),
             )
 
         residual = keep.tile([P, T], F32, name="residual", tag="scales_then_residual")
         for a, r in MOVES_AHEAD_OF_RT:
-            move_scales(a, r)
+            move_scales(a, r, PLANES[0])
         nc.sync.dma_start(residual[:, 0:RT_SPLIT], rT[:, 0:RT_SPLIT])
         for a, r in MOVES_INSIDE_RT:
-            move_scales(a, r)
+            move_scales(a, r, PLANES[0])
         nc.sync.dma_start(residual[:, RT_SPLIT:T], rT[:, RT_SPLIT:T])
+        for a in range(PASSES):
+            for r in range(QUAD_ROWS):
+                move_scales(a, r, PLANES[1])
 
         def read_by_lines(source):
             return source.rearrange("p i (c j) -> p c i j", j=LINE)
@@ -144,6 +152,7 @@ def tile_list_tabres_gelu_kernel(tc, tab_words, tab_scales, w, rT, b, offs, out)
         activated = []
         for col in range(0, S, BANK):
             acc = psum.tile([M, BANK], F32, name="acc", bufs=SUM_BANKS)
+            first = max(start for start, count in PLANES if start <= col)
             for a in range(PASSES):
                 for part in range(PARTS):
                     w_cols = slice((PARTS * a + part) * M, (PARTS * a + part + 1) * M)
@@ -152,7 +161,7 @@ def tile_list_tabres_gelu_kernel(tc, tab_words, tab_scales, w, rT, b, offs, out)
                         lhsT=w_codes[:, w_cols].bitcast(FP8X4),
                         lhsT_scale=w_scales[:, w_cols],
                         rhs=picked[a][:, col : col + BANK].bitcast(FP8X4),
-                        rhs_scale=v_scales[a][QUAD_ROWS * a : P, col : col + BANK],
+                        rhs_scale=v_scales[a, first][QUAD_ROWS * a : P, col - first : col - first + BANK],
                         start=(a == 0 and part == 0),
                         stop=(a == PASSES - 1 and part == PARTS - 1),
                     )

@@ -35,14 +35,15 @@ KIB = 1024
 UPPER_AT = (0, 3 * KIB)
 HI_AT = (4 * KIB, 13 * KIB)
 PICKED_AT = (5 * KIB, 13 * KIB)
-GATHER_WIDTHS = (S, S // 2)
+WORD_PIECES = ((S,), (1280, 768))
 MOVES_AHEAD_OF_RT = ((0, 0), (1, 0), (0, 1), (1, 1), (0, 2), (0, 3))
 MOVES_INSIDE_RT = ((1, 2), (1, 3))
-PLANES = ((0, S - BANK), (S - BANK, BANK))
+PLANES = ((0, S - 256), (S - 256, 256))
 RT_SPLIT = 3 * T // 8
-SUM_BANKS = 2
-OUT_WIDTHS = (512, 512, 512, 384, 128)
-OUT_STORES = (2, 2, 1, 1, 1)
+SUM_WIDTHS = (256, 128, 128, 512, 256, 512, 256)
+SUM_BANKS = 4
+OUT_WIDTHS = (512, 768, 512, 256)
+OUT_STORES = (2, 3, 1, 1)
 
 
 def tile_list_tabres_gelu_kernel(tc, tab_words, tab_scales, w, rT, b, offs, out):
@@ -63,11 +64,12 @@ def tile_list_tabres_gelu_kernel(tc, tab_words, tab_scales, w, rT, b, offs, out)
         nc.vector.memset(scale_table[0:FIRST_ROW, :].bitcast(I32), 0)
         bias_row = keep.tile([P, M], F32, name="bias_row")
         nc.gpsimd.memset(bias_row[0 : P - 1, :], 0.0)
-        nc.scalar.dma_start(bias_row[P - 1 : P, :], b.rearrange("(o n) -> o n", o=1))
         w_raw = [keep.tile([P, PACK, M], F32, name="w_raw%d" % a) for a in range(PASSES)]
         word_tables = [keep.tile([P, T], I32, name="word_table%d" % a) for a in range(PASSES)]
         for a in range(PASSES):
             nc.sync.dma_start(w_raw[a][:], w.rearrange("(a p i) n -> a p i n", a=PASSES, i=PACK)[a])
+            if a == 0:
+                nc.sync.dma_start(bias_row[P - 1 : P, :], b.rearrange("(o n) -> o n", o=1))
             nc.sync.dma_start(word_tables[a][:], tab_words[a].rearrange("p t i -> p (t i)").bitcast(I32))
 
         identity = keep.tile([P, P], F32, name="identity")
@@ -142,39 +144,39 @@ def tile_list_tabres_gelu_kernel(tc, tab_words, tab_scales, w, rT, b, offs, out)
                 in_=parts[:].rearrange("p h n i -> p (h n i)"),
             )
             words = shared.tile([P, S], U32, name="picked%d" % a, offset=PICKED_AT[a], align_bytes=64)
-            count = GATHER_WIDTHS[a]
-            for first in range(0, S, count):
+            first = 0
+            for count in WORD_PIECES[a]:
                 nc.vector.tensor_copy(
                     words[:, first : first + count], word_tables[a][:].bitcast(U32).indirect(entries(first, count))
                 )
+                first = first + count
             picked.append(words)
 
-        activated = []
-        for col in range(0, S, BANK):
+        activated = keep.tile([M, S], F32, name="activated")
+        col = 0
+        for width in SUM_WIDTHS:
             acc = psum.tile([M, BANK], F32, name="acc", bufs=SUM_BANKS)
             first = max(start for start, count in PLANES if start <= col)
             for a in range(PASSES):
                 for part in range(PARTS):
                     w_cols = slice((PARTS * a + part) * M, (PARTS * a + part + 1) * M)
                     nc.tensor.matmul_mx(
-                        out=acc[:],
+                        out=acc[:, 0:width],
                         lhsT=w_codes[:, w_cols].bitcast(FP8X4),
                         lhsT_scale=w_scales[:, w_cols],
-                        rhs=picked[a][:, col : col + BANK].bitcast(FP8X4),
-                        rhs_scale=v_scales[a, first][QUAD_ROWS * a : P, col - first : col - first + BANK],
+                        rhs=picked[a][:, col : col + width].bitcast(FP8X4),
+                        rhs_scale=v_scales[a, first][QUAD_ROWS * a : P, col - first : col - first + width],
                         start=(a == 0 and part == 0),
                         stop=(a == PASSES - 1 and part == PARTS - 1),
                     )
-            gelu = keep.tile([M, BANK], F32, name="gelu%d" % col)
-            nc.scalar.activation(gelu[:], acc[:], ACT.Gelu_apprx_tanh, bias=bias[:])
-            activated.append(gelu)
+            nc.scalar.activation(activated[:, col : col + width], acc[:, 0:width], ACT.Gelu_apprx_tanh, bias=bias[:])
+            col = col + width
 
         col = 0
         for width, stores in zip(OUT_WIDTHS, OUT_STORES):
-            bank, inner = divmod(col, BANK)
             result = keep.tile([M, width], F32, name="result%d" % col)
             nc.vector.tensor_tensor(
-                result[:], residual[:].indirect(entries(col, width)), activated[bank][:, inner : inner + width], ALU.add
+                result[:], residual[:].indirect(entries(col, width)), activated[:, col : col + width], ALU.add
             )
             step = width // stores
             for done in range(0, width, step):

@@ -82,8 +82,6 @@ def tile_list_tabres_gelu_kernel(tc, tab_words, tab_scales, w, rT, b, offs, out)
                 v_scales[a, first] = plane
         bias_turned = psum.tile([M, P], F32, name="bias_turned")
         nc.tensor.transpose(bias_turned[:], bias_row[:], identity[:])
-        bias = keep.tile([M, 1], F32, name="bias")
-        nc.scalar.copy(bias[:], bias_turned[:, P - 1 : P])
 
         picked_scales = keep.tile([P, S], U8, name="picked_scales")
         nc.vector.tensor_copy(picked_scales[:], scale_table[:].indirect(offsets[:]))
@@ -119,7 +117,7 @@ def tile_list_tabres_gelu_kernel(tc, tab_words, tab_scales, w, rT, b, offs, out)
         runs = [slice(h * M // RUNS, (h + 1) * M // RUNS) for h in range(RUNS)]
         for a in range(PASSES):
             upper = shared.tile([P, PACK, M], F32, name="upper%d" % a, offset=UPPER_AT[a], align_bytes=64)
-            kept = keep.tile([P, PACK, M], U32, name="kept%d" % a)
+            kept = keep.tile([P, PACK, M], U32, name="kept%d" % a, tag="kept%d" % a)
             hi = shared.tile([P, PACK, M], F32, name="hi%d" % a, offset=HI_AT[a], align_bytes=64)
             parts = keep.tile([P, PARTS, M, PACK], BF16, name="parts%d" % a, align_bytes=64)
             halves = w_raw[a][:].bitcast(BF16)
@@ -152,6 +150,8 @@ def tile_list_tabres_gelu_kernel(tc, tab_words, tab_scales, w, rT, b, offs, out)
                 first = first + count
             picked.append(words)
 
+        bias = keep.tile([M, 1], F32, name="bias", tag="kept0")
+        nc.scalar.copy(bias[:], bias_turned[:, P - 1 : P])
         activated = keep.tile([M, S], F32, name="activated")
         col = 0
         for width in SUM_WIDTHS:

@@ -35,15 +35,15 @@ KIB = 1024
 UPPER_AT = (0, 3 * KIB)
 HI_AT = (4 * KIB, 13 * KIB)
 PICKED_AT = (5 * KIB, 13 * KIB)
-WORD_PIECES = ((S,), (1280, 768))
+WORD_PIECES = ((S,), (S // 2, S // 2))
 MOVES_AHEAD_OF_RT = ((0, 0), (1, 0), (0, 1), (1, 1), (0, 2), (0, 3))
 MOVES_INSIDE_RT = ((1, 2), (1, 3))
 PLANES = ((0, S - 256), (S - 256, 256))
 RT_SPLIT = 3 * T // 8
-SUM_WIDTHS = (256, 128, 128, 512, 256, 512, 256)
+SUM_WIDTHS = (256, 128, 128, 512, 256, 256, 256, 256)
 SUM_BANKS = 4
-OUT_WIDTHS = (512, 768, 512, 256)
-OUT_STORES = (2, 3, 1, 1)
+OUT_WIDTHS = (512, 512, 512, 384, 128)
+OUT_STORES = (2, 2, 1, 1, 1)
 
 
 def tile_list_tabres_gelu_kernel(tc, tab_words, tab_scales, w, rT, b, offs, out):

@@ -38,9 +38,8 @@ PICKED_AT = (5 * KIB, 13 * KIB)
 WORD_PIECES = ((S,), (S // 2, S // 2))
 MOVES_AHEAD_OF_RT = ((0, 0), (1, 0), (0, 1), (1, 1), (0, 2), (0, 3))
 MOVES_INSIDE_RT = ((1, 2), (1, 3))
-PLANES = ((0, S - 256), (S - 256, 256))
 RT_SPLIT = 3 * T // 8
-SUM_WIDTHS = (256, 128, 128, 512, 256, 256, 256, 256)
+SUM_WIDTHS = (256, 128, 128, 512, 512, 512)
 SUM_BANKS = 4
 OUT_WIDTHS = (512, 512, 512, 384, 128)
 OUT_STORES = (2, 2, 1, 1, 1)
@@ -74,36 +73,29 @@ def tile_list_tabres_gelu_kernel(tc, tab_words, tab_scales, w, rT, b, offs, out)
 
         identity = keep.tile([P, P], F32, name="identity")
         make_identity(nc, identity[:])
-        v_scales = {}
-        for first, count in PLANES:
-            for a in range(PASSES):
-                plane = keep.tile([P, count], U8, name="v_scales%d_%d" % (a, first), align_bytes=64)
-                nc.gpsimd.memset(plane[:].bitcast(I32), 0)
-                v_scales[a, first] = plane
+        v_scales = [keep.tile([P, S], U8, name="v_scales%d" % a, align_bytes=64) for a in range(PASSES)]
+        for plane in v_scales:
+            nc.gpsimd.memset(plane[:].bitcast(I32), 0)
         bias_turned = psum.tile([M, P], F32, name="bias_turned")
         nc.tensor.transpose(bias_turned[:], bias_row[:], identity[:])
 
         picked_scales = keep.tile([P, S], U8, name="picked_scales")
         nc.vector.tensor_copy(picked_scales[:], scale_table[:].indirect(offsets[:]))
 
-        def move_scales(a, r, columns):
-            first, count = columns
+        def move_scales(a, r):
             pass_first = FIRST_ROW + PASS_ROWS * a
             nc.sync.dma_start(
-                v_scales[a, first][QUAD_ROWS * a + r : P : QUADRANT, :].bitcast(I32),
-                picked_scales[pass_first + r : pass_first + PASS_ROWS : QUAD_ROWS, first : first + count].bitcast(I32),
+                v_scales[a][QUAD_ROWS * a + r : P : QUADRANT, :].bitcast(I32),
+                picked_scales[pass_first + r : pass_first + PASS_ROWS : QUAD_ROWS, :].bitcast(I32),
             )
 
         residual = keep.tile([P, T], F32, name="residual", tag="scales_then_residual")
         for a, r in MOVES_AHEAD_OF_RT:
-            move_scales(a, r, PLANES[0])
+            move_scales(a, r)
         nc.sync.dma_start(residual[:, 0:RT_SPLIT], rT[:, 0:RT_SPLIT])
         for a, r in MOVES_INSIDE_RT:
-            move_scales(a, r, PLANES[0])
+            move_scales(a, r)
         nc.sync.dma_start(residual[:, RT_SPLIT:T], rT[:, RT_SPLIT:T])
-        for a in range(PASSES):
-            for r in range(QUAD_ROWS):
-                move_scales(a, r, PLANES[1])
 
         def read_by_lines(source):
             return source.rearrange("p i (c j) -> p c i j", j=LINE)
@@ -156,7 +148,6 @@ def tile_list_tabres_gelu_kernel(tc, tab_words, tab_scales, w, rT, b, offs, out)
         col = 0
         for width in SUM_WIDTHS:
             acc = psum.tile([M, BANK], F32, name="acc", bufs=SUM_BANKS)
-            first = max(start for start, count in PLANES if start <= col)
             for a in range(PASSES):
                 for part in range(PARTS):
                     w_cols = slice((PARTS * a + part) * M, (PARTS * a + part + 1) * M)
@@ -165,7 +156,7 @@ def tile_list_tabres_gelu_kernel(tc, tab_words, tab_scales, w, rT, b, offs, out)
                         lhsT=w_codes[:, w_cols].bitcast(FP8X4),
                         lhsT_scale=w_scales[:, w_cols],
                         rhs=picked[a][:, col : col + width].bitcast(FP8X4),
-                        rhs_scale=v_scales[a, first][QUAD_ROWS * a : P, col - first : col - first + width],
+                        rhs_scale=v_scales[a][QUAD_ROWS * a : P, col : col + width],
                         start=(a == 0 and part == 0),
                         stop=(a == PASSES - 1 and part == PARTS - 1),
                     )

@@ -38,6 +38,7 @@ PICKED_AT = (5 * KIB, 13 * KIB)
 WORD_PIECES = ((S,), (S // 2, S // 2))
 MOVES_AHEAD_OF_RT = ((0, 0), (1, 0), (0, 1), (1, 1), (0, 2), (0, 3))
 MOVES_INSIDE_RT = ((1, 2), (1, 3))
+PLANES = ((0, S - BANK), (S - BANK, BANK))
 RT_SPLIT = 3 * T // 8
 SUM_WIDTHS = (256, 128, 128, 512, 512, 512)
 SUM_BANKS = 4
@@ -73,29 +74,36 @@ def tile_list_tabres_gelu_kernel(tc, tab_words, tab_scales, w, rT, b, offs, out)
 
         identity = keep.tile([P, P], F32, name="identity")
         make_identity(nc, identity[:])
-        v_scales = [keep.tile([P, S], U8, name="v_scales%d" % a, align_bytes=64) for a in range(PASSES)]
-        for plane in v_scales:
-            nc.gpsimd.memset(plane[:].bitcast(I32), 0)
+        v_scales = {}
+        for first, count in PLANES:
+            for a in range(PASSES):
+                plane = keep.tile([P, count], U8, name="v_scales%d_%d" % (a, first), align_bytes=64)
+                nc.gpsimd.memset(plane[:].bitcast(I32), 0)
+                v_scales[a, first] = plane
         bias_turned = psum.tile([M, P], F32, name="bias_turned")
         nc.tensor.transpose(bias_turned[:], bias_row[:], identity[:])
 
         picked_scales = keep.tile([P, S], U8, name="picked_scales")
         nc.vector.tensor_copy(picked_scales[:], scale_table[:].indirect(offsets[:]))
 
-        def move_scales(a, r):
+        def move_scales(a, r, columns):
+            first, count = columns
             pass_first = FIRST_ROW + PASS_ROWS * a
             nc.sync.dma_start(
-                v_scales[a][QUAD_ROWS * a + r : P : QUADRANT, :].bitcast(I32),
-                picked_scales[pass_first + r : pass_first + PASS_ROWS : QUAD_ROWS, :].bitcast(I32),
+                v_scales[a, first][QUAD_ROWS * a + r : P : QUADRANT, :].bitcast(I32),
+                picked_scales[pass_first + r : pass_first + PASS_ROWS : QUAD_ROWS, first : first + count].bitcast(I32),
             )
 
         residual = keep.tile([P, T], F32, name="residual", tag="scales_then_residual")
         for a, r in MOVES_AHEAD_OF_RT:
-            move_scales(a, r)
+            move_scales(a, r, PLANES[0])
         nc.sync.dma_start(residual[:, 0:RT_SPLIT], rT[:, 0:RT_SPLIT])
         for a, r in MOVES_INSIDE_RT:
-            move_scales(a, r)
+            move_scales(a, r, PLANES[0])
         nc.sync.dma_start(residual[:, RT_SPLIT:T], rT[:, RT_SPLIT:T])
+        for a in range(PASSES):
+            for r in range(QUAD_ROWS):
+                move_scales(a, r, PLANES[1])
 
         def read_by_lines(source):
             return source.rearrange("p i (c j) -> p c i j", j=LINE)
@@ -148,6 +156,7 @@ def tile_list_tabres_gelu_kernel(tc, tab_words, tab_scales, w, rT, b, offs, out)
         col = 0
         for width in SUM_WIDTHS:
             acc = psum.tile([M, BANK], F32, name="acc", bufs=SUM_BANKS)
+            first = max(start for start, count in PLANES if start <= col)
             for a in range(PASSES):
                 for part in range(PARTS):
                     w_cols = slice((PARTS * a + part) * M, (PARTS * a + part + 1) * M)
@@ -156,7 +165,7 @@ def tile_list_tabres_gelu_kernel(tc, tab_words, tab_scales, w, rT, b, offs, out)
                         lhsT=w_codes[:, w_cols].bitcast(FP8X4),
                         lhsT_scale=w_scales[:, w_cols],
                         rhs=picked[a][:, col : col + width].bitcast(FP8X4),
-                        rhs_scale=v_scales[a][QUAD_ROWS * a : P, col : col + width],
+                        rhs_scale=v_scales[a, first][QUAD_ROWS * a : P, col - first : col - first + width],
                         start=(a == 0 and part == 0),
                         stop=(a == PASSES - 1 and part == PARTS - 1),
                     )

@@ -40,9 +40,9 @@ MOVES_AHEAD_OF_RT = ((0, 0), (1, 0), (0, 1), (1, 1), (0, 2), (0, 3))
 MOVES_INSIDE_RT = ((1, 2), (1, 3))
 PLANES = ((0, S - BANK), (S - BANK, BANK))
 RT_SPLIT = 3 * T // 8
-SUM_WIDTHS = (256, 128, 128, 512, 512, 512)
+SUM_WIDTHS = (256, 128, 128, 512, 512, 256, 256)
 SUM_BANKS = 4
-OUT_WIDTHS = (512, 512, 512, 384, 128)
+OUT_WIDTHS = (512, 512, 512, 256, 256)
 OUT_STORES = (2, 2, 1, 1, 1)
 
 

@@ -68,7 +68,7 @@ def tile_list_tabres_gelu_kernel(tc, tab_words, tab_scales, w, rT, b, offs, out)
         word_tables = [keep.tile([P, T], I32, name="word_table%d" % a) for a in range(PASSES)]
         for a in range(PASSES):
             nc.sync.dma_start(w_raw[a][:], w.rearrange("(a p i) n -> a p i n", a=PASSES, i=PACK)[a])
-            if a == 0:
+            if a == PASSES - 1:
                 nc.sync.dma_start(bias_row[P - 1 : P, :], b.rearrange("(o n) -> o n", o=1))
             nc.sync.dma_start(word_tables[a][:], tab_words[a].rearrange("p t i -> p (t i)").bitcast(I32))
 

from contextlib import ExitStack

import concourse.mybir as mybir
from concourse.masks import make_identity

K, M, T, S = 1024, 128, 4096, 2048
FLOPS = 2 * 2 * K * M * S
BYTES = K * T + (K // 32) * T + 4 * K * M + 4 * M * T + 4 * M + 2 * 128 * (S // 16) + 4 * M * S

F32 = mybir.dt.float32
BF16 = mybir.dt.bfloat16
I32 = mybir.dt.int32
U32 = mybir.dt.uint32
U16 = mybir.dt.uint16
U8 = mybir.dt.uint8
FP8X4 = mybir.dt.float8_e4m3fn_x4
ALU = mybir.AluOpType
ACT = mybir.ActivationFunctionType

P = 128
PACK = 4
PASSES = K // (P * PACK)
PARTS = 2
BANK = 512
GROUP = 16
QUADRANT = 32
QUAD_ROWS = 4
PASS_ROWS = 16
FIRST_ROW = P - PASSES * PASS_ROWS
KEPT_BIT = float(1 << 20)
FLOOR_SHIFT = -15.0 / 32.0
RUNS = 4
LINE = 4
KIB = 1024
UPPER_AT = (0, 3 * KIB)
HI_AT = (4 * KIB, 13 * KIB)
PICKED_AT = (5 * KIB, 13 * KIB)
WORD_PIECES = ((S,), (S // 2, S // 2))
MOVES_AHEAD_OF_RT = ((0, 0), (1, 0), (0, 1), (1, 1), (0, 2), (0, 3))
MOVES_INSIDE_RT = ((1, 2), (1, 3))
PLANES = ((0, S - BANK), (S - BANK, BANK))
RT_SPLIT = 3 * T // 8
SUM_WIDTHS = (256, 128, 128, 512, 512, 256, 256)
SUM_BANKS = 4
OUT_WIDTHS = (512, 512, 512, 256, 256)
OUT_STORES = (2, 2, 1, 1, 1)


def tile_list_tabres_gelu_kernel(tc, tab_words, tab_scales, w, rT, b, offs, out):
    nc = tc.nc
    with ExitStack() as ctx:
        keep = ctx.enter_context(tc.tile_pool(name="keep", bufs=1))
        shared = ctx.enter_context(tc.tile_pool(name="shared", bufs=1))
        psum = ctx.enter_context(tc.psum_pool(name="psum", bufs=1))

        offsets = keep.tile([P, S // GROUP], U16, name="offsets")

        def entries(first, count):
            return offsets[:, first // GROUP : (first + count) // GROUP]

        scale_table = keep.tile([P, T], U8, name="scale_table", tag="scales_then_residual")
        nc.sync.dma_start(scale_table[FIRST_ROW:P, :].bitcast(I32), tab_scales.bitcast(I32).rearrange("a q t -> (a q) t"))
        nc.sync.dma_start(offsets[:], offs)
        nc.vector.memset(scale_table[0:FIRST_ROW, :].bitcast(I32), 0)
        bias_row = keep.tile([P, M], F32, name="bias_row")
        nc.gpsimd.memset(bias_row[0 : P - 1, :], 0.0)
        w_raw = [keep.tile([P, PACK, M], F32, name="w_raw%d" % a) for a in range(PASSES)]
        word_tables = [keep.tile([P, T], I32, name="word_table%d" % a) for a in range(PASSES)]
        for a in range(PASSES):
            nc.sync.dma_start(w_raw[a][:], w.rearrange("(a p i) n -> a p i n", a=PASSES, i=PACK)[a])
            if a == PASSES - 1:
                nc.sync.dma_start(bias_row[P - 1 : P, :], b.rearrange("(o n) -> o n", o=1))
            nc.sync.dma_start(word_tables[a][:], tab_words[a].rearrange("p t i -> p (t i)").bitcast(I32))

        identity = keep.tile([P, P], F32, name="identity")
        make_identity(nc, identity[:])
        v_scales = {}
        for first, count in PLANES:
            for a in range(PASSES):
                plane = keep.tile([P, count], U8, name="v_scales%d_%d" % (a, first), align_bytes=64)
                nc.gpsimd.memset(plane[:].bitcast(I32), 0)
                v_scales[a, first] = plane
        bias_turned = psum.tile([M, P], F32, name="bias_turned")
        nc.tensor.transpose(bias_turned[:], bias_row[:], identity[:])

        picked_scales = keep.tile([P, S], U8, name="picked_scales")
        nc.vector.tensor_copy(picked_scales[:], scale_table[:].indirect(offsets[:]))

        def move_scales(a, r, columns):
            first, count = columns
            pass_first = FIRST_ROW + PASS_ROWS * a
            nc.sync.dma_start(
                v_scales[a, first][QUAD_ROWS * a + r : P : QUADRANT, :].bitcast(I32),
                picked_scales[pass_first + r : pass_first + PASS_ROWS : QUAD_ROWS, first : first + count].bitcast(I32),
            )

        residual = keep.tile([P, T], F32, name="residual", tag="scales_then_residual")
        for a, r in MOVES_AHEAD_OF_RT:
            move_scales(a, r, PLANES[0])
        nc.sync.dma_start(residual[:, 0:RT_SPLIT], rT[:, 0:RT_SPLIT])
        for a, r in MOVES_INSIDE_RT:
            move_scales(a, r, PLANES[0])
        nc.sync.dma_start(residual[:, RT_SPLIT:T], rT[:, RT_SPLIT:T])
        for a in range(PASSES):
            for r in range(QUAD_ROWS):
                move_scales(a, r, PLANES[1])

        def read_by_lines(source):
            return source.rearrange("p i (c j) -> p c i j", j=LINE)

        def write_by_lines(target):
            return target.rearrange("p (c j) i -> p c i j", j=LINE)

        w_codes = keep.tile([P, PASSES * PARTS * M], U32, name="w_codes", align_bytes=64)
        w_scales = keep.tile([P, PASSES * PARTS * M], U8, name="w_scales", align_bytes=64)
        picked = []
        runs = [slice(h * M // RUNS, (h + 1) * M // RUNS) for h in range(RUNS)]
        for a in range(PASSES):
            upper = shared.tile([P, PACK, M], F32, name="upper%d" % a, offset=UPPER_AT[a], align_bytes=64)
            kept = keep.tile([P, PACK, M], U32, name="kept%d" % a, tag="kept%d" % a)
            hi = shared.tile([P, PACK, M], F32, name="hi%d" % a, offset=HI_AT[a], align_bytes=64)
            parts = keep.tile([P, PARTS, M, PACK], BF16, name="parts%d" % a, align_bytes=64)
            halves = w_raw[a][:].bitcast(BF16)
            for run in runs:
                nc.scalar.activation(upper[:, :, run], halves[:, :, 2 * run.start + 1 : 2 * run.stop : 2], ACT.Copy)
                nc.scalar.activation(
                    kept[:, :, run], upper[:, :, run].bitcast(U32), ACT.Copy, scale=1.0 / KEPT_BIT, bias=FLOOR_SHIFT
                )
                nc.scalar.activation(hi[:, :, run].bitcast(U32), kept[:, :, run], ACT.Copy, scale=KEPT_BIT)
                nc.gpsimd.tensor_tensor(
                    write_by_lines(parts[:, 1, run, :]),
                    read_by_lines(w_raw[a][:, :, run]),
                    read_by_lines(hi[:, :, run]),
                    ALU.subtract,
                )
            for run in runs:
                nc.scalar.copy(write_by_lines(parts[:, 0, run, :]), read_by_lines(hi[:, :, run]))
            pass_cols = slice(PARTS * a * M, PARTS * (a + 1) * M)
            nc.vector.quantize_mx(
                out=w_codes[:, pass_cols].bitcast(FP8X4),
                scales=w_scales[:, pass_cols],
                in_=parts[:].rearrange("p h n i -> p (h n i)"),
            )
            words = shared.tile([P, S], U32, name="picked%d" % a, offset=PICKED_AT[a], align_bytes=64)
            first = 0
            for count in WORD_PIECES[a]:
                nc.vector.tensor_copy(
                    words[:, first : first + count], word_tables[a][:].bitcast(U32).indirect(entries(first, count))
                )
                first = first + count
            picked.append(words)

        bias = keep.tile([M, 1], F32, name="bias", tag="kept0")
        nc.scalar.copy(bias[:], bias_turned[:, P - 1 : P])
        activated = keep.tile([M, S], F32, name="activated")
        col = 0
        for width in SUM_WIDTHS:
            acc = psum.tile([M, BANK], F32, name="acc", bufs=SUM_BANKS)
            first = max(start for start, count in PLANES if start <= col)
            for a in range(PASSES):
                for part in range(PARTS):
                    w_cols = slice((PARTS * a + part) * M, (PARTS * a + part + 1) * M)
                    nc.tensor.matmul_mx(
                        out=acc[:, 0:width],
                        lhsT=w_codes[:, w_cols].bitcast(FP8X4),
                        lhsT_scale=w_scales[:, w_cols],
                        rhs=picked[a][:, col : col + width].bitcast(FP8X4),
                        rhs_scale=v_scales[a, first][QUAD_ROWS * a : P, col - first : col - first + width],
                        start=(a == 0 and part == 0),
                        stop=(a == PASSES - 1 and part == PARTS - 1),
                    )
            nc.scalar.activation(activated[:, col : col + width], acc[:, 0:width], ACT.Gelu_apprx_tanh, bias=bias[:])
            col = col + width

        col = 0
        for width, stores in zip(OUT_WIDTHS, OUT_STORES):
            result = keep.tile([M, width], F32, name="result%d" % col)
            nc.vector.tensor_tensor(
                result[:], residual[:].indirect(entries(col, width)), activated[:, col : col + width], ALU.add
            )
            step = width // stores
            for done in range(0, width, step):
                nc.sync.dma_start(out[:, col + done : col + done + step], result[:, done : done + step])
            col = col + width
